import numpy as np
import ml_dtypes


def mxq(x, axis, fmt="e4m3"):
    dtype, down = {"e4m3": (ml_dtypes.float8_e4m3fn, 7), "e5m2": (ml_dtypes.float8_e5m2, 14)}[fmt]
    v = np.moveaxis(np.asarray(x, np.float32).astype(ml_dtypes.bfloat16).astype(np.float64), axis, -1)
    blocks = v.reshape(v.shape[:-1] + (-1, 32))
    amax = np.abs(blocks).max(-1, keepdims=True)
    byte = np.maximum(np.where(amax > 0, np.frexp(amax)[1] - 1 + 127, 0) - down, 1)
    scale = np.exp2(byte - 127.0)
    codes = (blocks / scale).astype(np.float32).astype(dtype).astype(np.float64)
    return np.moveaxis((codes * scale).reshape(v.shape), -1, axis)


WIDE = False


def mx_kscale(k):
    if not WIDE:
        return np.ones(k)
    levels = np.array([10, -10, 5, -5, 0])
    if k % 512:
        return np.exp2(np.random.permutation(np.resize(levels, k // 32))).repeat(32)
    a = np.empty((k // 512, 16))
    for p in range(k // 512):
        a[p, :8] = np.random.permutation(np.resize(levels, 8))
        for g in range(8):
            far = levels[np.abs(levels - a[p, g]) >= 10]
            a[p, g + 8] = far[np.random.randint(len(far))]
    return np.exp2(a.ravel()).repeat(32)


BF16 = ml_dtypes.bfloat16


def bf(x):
    return np.asarray(x, np.float32).astype(BF16)


def f64(x):
    return np.asarray(x).astype(np.float64)

E4M3FN = np.array([(-1.0 if i & 128 else 1.0) * ((1.0 + (i & 7) / 8.0) * 2.0 ** (((i >> 3) & 15) - 7) if i & 120 else (i & 7) * 2.0 ** -9) for i in range(256)])


def e4m3fn_bytes(y):
    return np.clip(np.asarray(y, np.float64), -448.0, 448.0).astype(np.float32).astype(ml_dtypes.float8_e4m3fn).view(np.uint8)


def e4m3fn_values(b):
    return E4M3FN[b]

def planes(Y):
    n, m = Y.shape
    b = f64(bf(Y)).reshape(n // 32, 32, m)
    amax = np.abs(b).max(1)
    byte = np.clip(np.where(amax > 0, np.frexp(amax)[1] - 1 + 127 - 7, 1), 1, 254)
    codes = (b * np.exp2(127.0 - byte)[:, None, :]).reshape(n, m).astype(np.float32).astype(ml_dtypes.float8_e4m3fn).view(np.uint8)
    words = codes.reshape(n // 512, 128, 4, m).transpose(0, 1, 3, 2)
    return np.ascontiguousarray(words), np.ascontiguousarray(byte.astype(np.uint8).reshape(n // 512, 16, m))


T, K, N, BLK = 1024, 1536, 1024, 128

FP8_MAX = 448.0
CONTRAST = 0.3
SPREAD = 0.8
BIAS = 0.4

def setup_inputs():
    s = mx_kscale(K)
    contrast = np.exp(CONTRAST * np.random.randn(T, 1))
    X = contrast * np.random.randn(T, K) * s[None, :]
    X_scale = (np.abs(X).reshape(T, K // BLK, BLK).max(axis=2) / FP8_MAX).astype(np.float32)
    X_bytes = e4m3fn_bytes(X / np.repeat(f64(X_scale), BLK, axis=1))
    unit = np.exp(SPREAD * np.random.randn(N))
    W1 = np.random.randn(K, N) * unit[None, :] / np.sqrt(K) / s[:, None]
    W2 = np.random.randn(K, N) * unit[None, :] / np.sqrt(K) / s[:, None]
    b1 = BIAS * np.random.randn(N) * unit
    b2 = BIAS * np.random.randn(N) * unit
    return {"X_bytes": X_bytes, "X_scale": X_scale, "W1": bf(W1), "W2": bf(W2), "b1": bf(b1), "b2": bf(b2)}

def reference(X_bytes, X_scale, W1, W2, b1, b2):
    X = e4m3fn_values(X_bytes) * np.repeat(f64(X_scale), BLK, axis=1)
    Xq = mxq(X, 1, "e4m3")
    h1 = (Xq @ mxq(f64(W1), 0, "e4m3")) + f64(b1)[None, :]
    h2 = (Xq @ mxq(f64(W2), 0, "e4m3")) + f64(b2)[None, :]
    y = np.maximum(h1, h2)
    Y = y.T
    words, scales = planes(Y)
    return y, words, scales

@@ -1,0 +1,370 @@
+from contextlib import ExitStack
+
+import concourse.mybir as mybir
+from concourse.masks import make_identity
+
+T, K, N = 1024, 1536, 1024
+FLOPS = 2 * T * K * 2 * N
+
+F32 = mybir.dt.float32
+BF16 = mybir.dt.bfloat16
+U32 = mybir.dt.uint32
+I32 = mybir.dt.int32
+U8 = mybir.dt.uint8
+FP8 = mybir.dt.float8_e4m3fn
+FP8X4 = mybir.dt.float8_e4m3fn_x4
+ALU = mybir.AluOpType
+ACT = mybir.ActivationFunctionType
+
+P = 128
+PACK = 4
+SPAN = P * PACK
+PASSES = K // SPAN
+BLOCKS = K // P
+
+
+def tile_maxout_patch_layer_b1_kernel(tc, X_bytes, X_scale, W1, W2, b1, b2, out_0, out_1, out_2):
+    nc = tc.nc
+    weights = (W1, W2)
+    biases = (b1, b2)
+
+    with ExitStack() as ctx:
+        keep = ctx.enter_context(tc.tile_pool(name="keep", bufs=1))
+        work = ctx.enter_context(tc.tile_pool(name="work", bufs=3))
+        psum = ctx.enter_context(tc.psum_pool(name="psum", bufs=1))
+        ctx.enter_context(tc.manual_schedule())
+
+        tiles = {}
+
+        def copy_on(engine, out, in_):
+            if engine == "V":
+                nc.vector.tensor_copy(out=out, in_=in_)
+            else:
+                nc.scalar.copy(out=out, in_=in_)
+
+        def load_scales():
+            xs = keep.tile([P, T // P, BLOCKS], F32, name="x_scale")
+            nc.sync.dma_start(out=xs[:], in_=X_scale.rearrange("(i p) j -> p i j", p=P))
+            tiles["xs"] = xs
+
+        def load_x(h, b):
+            xb = keep.tile([P, 2, K], U8, name="x_bytes_%d_%d" % (h, b))
+            first = SPAN * h + 2 * P * b
+            nc.sync.dma_start(out=xb[:], in_=X_bytes[first : first + 2 * P, :].rearrange("(i p) k -> p i k", p=P))
+            tiles["xb", h, b] = xb
+
+        def load_w(g, w, c):
+            raw = keep.tile([P, PACK, SPAN], BF16, name="w_raw_%d_%d_%d" % (g, w, c))
+            rows = weights[w][SPAN * c : SPAN * (c + 1), SPAN * g : SPAN * (g + 1)]
+            nc.sync.dma_start(out=raw[:], in_=rows.rearrange("(p j) n -> p j n", j=PACK))
+            tiles["wraw", g, w, c] = raw
+
+        def load_bias(w):
+            raw = keep.tile([P, N // SPAN, PACK], BF16, name="bias_raw_%d" % w)
+            nc.sync.dma_start(out=raw[:], in_=biases[w].rearrange("(g p t) -> p g t", p=P, t=PACK))
+            bias = keep.tile([P, N // SPAN, PACK], F32, name="bias_%d" % w)
+            nc.gpsimd.tensor_copy(out=bias[:], in_=raw[:])
+            tiles["bias", w] = bias
+
+        def widen(h, jobs):
+            for c, i in jobs:
+                tiles["wide", h, c, i] = work.tile([P, SPAN], BF16, name="x_wide", bufs=8)
+            for q in range(4):
+                for c, i in jobs:
+                    j = 4 * c + q
+                    codes = tiles["xb", h, i // 2][:, i % 2, P * j : P * (j + 1)].bitcast(FP8)
+                    halves = tiles["wide", h, c, i][:].rearrange("p (u q r e) -> p q r u e", u=2, q=4, e=2)
+                    nc.vector.tensor_scalar(
+                        out=halves[:, q],
+                        in0=codes.rearrange("p (r u e) -> p r u e", u=2, e=2),
+                        scalar1=tiles["xs"][:, 4 * h + i, j : j + 1],
+                        scalar2=None,
+                        op0=ALU.mult,
+                    )
+
+        def turn_x(h, c, b):
+            bank = psum.tile([P, 2, 2, P], F32, name="turn", bufs=3)
+            for i in range(2):
+                words = tiles["wide", h, c, 2 * b + i][:].bitcast(F32)
+                for u in range(2):
+                    nc.tensor.transpose(bank[:, i, u, :], words[:, P * u : P * (u + 1)], ident[:])
+            tiles["xbank", h, c, b] = bank
+
+        def copy_x(h, c, b, engine):
+            if b == 0:
+                tiles["xgrp", h, c] = work.tile([P, 2, 2 * P * PACK], BF16, name="x_grouped", bufs=3, align_bytes=64)
+            words = tiles["xgrp", h, c][:, b, :].bitcast(F32).rearrange("p (i r u) -> p i r u", i=2, u=2)
+            copy_on(engine, words, tiles["xbank", h, c, b][:].rearrange("p i u r -> p i r u"))
+
+        def quantize(source, codes, scales):
+            nc.vector.quantize_mx(out=codes.bitcast(FP8X4), scales=scales, in_=source)
+
+        def quant_x(h, c, first=0, pairs=2):
+            if first == 0:
+                codes = keep.tile([P, SPAN], U32, name="x_codes_%d_%d" % (h, c), align_bytes=64)
+                scales = keep.tile([P, SPAN], U8, name="x_mxscales_%d_%d" % (h, c), align_bytes=64)
+                tiles["xq", h, c] = (codes, scales)
+            codes, scales = tiles["xq", h, c]
+            cols = slice(2 * P * first, 2 * P * (first + pairs))
+            source = tiles["xgrp", h, c][:, first : first + pairs, :].rearrange("p b f -> p (b f)")
+            quantize(source, codes[:, cols], scales[:, cols])
+
+        def mix_w(g, w, c, engine, lo=0, hi=64):
+            if ("wgrp", g, w, c) not in tiles:
+                tiles["wgrp", g, w, c] = work.tile([P, SPAN * PACK], BF16, name="w_grouped", bufs=4, align_bytes=64)
+            out = tiles["wgrp", g, w, c][:].rearrange("p (t a b j) -> p a t b j", t=PACK, b=2, j=PACK)
+            in_ = tiles["wraw", g, w, c][:].rearrange("p j (a b t) -> p a t b j", t=PACK, b=2)
+            copy_on(engine, out[:, lo:hi], in_[:, lo:hi])
+
+        def quant_w(g, w, c):
+            codes = keep.tile([P, SPAN], U32, name="w_codes_%d_%d_%d" % (g, w, c), align_bytes=64)
+            scales = keep.tile([P, SPAN], U8, name="w_mxscales_%d_%d_%d" % (g, w, c), align_bytes=64)
+            quantize(tiles["wgrp", g, w, c][:], codes[:], scales[:])
+            tiles["wq", g, w, c] = (codes, scales)
+
+        def multiply(g, h, w, t, c, step, cols=slice(0, SPAN)):
+            key = ("acc", g, h, w, t, cols.start)
+            if step == 0:
+                tiles[key] = psum.tile([P, SPAN], F32, name="acc", bufs=5)
+            w_codes, w_scales = tiles["wq", g, w, c]
+            x_codes, x_scales = tiles["xq", h, c]
+            units = slice(P * t, P * (t + 1))
+            nc.tensor.matmul_mx(
+                out=tiles[key][:, : cols.stop - cols.start],
+                lhsT=w_codes[:, units].bitcast(FP8X4),
+                lhsT_scale=w_scales[:, units],
+                rhs=x_codes[:, cols].bitcast(FP8X4),
+                rhs_scale=x_scales[:, cols],
+                start=(step == 0),
+                stop=(step == PASSES - 1),
+            )
+
+        def one_pass(g, h, w, c, step):
+            for t in range(PACK):
+                multiply(g, h, w, t, c, step)
+
+        def product(g, h, w, t, cols=slice(0, SPAN)):
+            for c in range(PASSES):
+                multiply(g, h, w, t, c, c, cols)
+
+        def first_piece(g, h, t, cols=slice(0, SPAN)):
+            if cols.start == 0:
+                tiles["piece", g, h, t] = work.tile([P, SPAN], F32, name="piece", bufs=8)
+            nc.scalar.activation(
+                out=tiles["piece", g, h, t][:, cols],
+                in_=tiles["acc", g, h, 0, t, cols.start][:, : cols.stop - cols.start],
+                func=ACT.Identity,
+                bias=tiles["bias", 0][:, g, t : t + 1],
+            )
+
+        def maxout(g, h, t, cols=slice(0, SPAN)):
+            width = cols.stop - cols.start
+            if t == 0:
+                y_units = work.tile([P, PACK, width], F32, name="y_units_%d_%d_%d" % (g, h, cols.start), bufs=1)
+                for i in range(cols.start // P, cols.stop // P):
+                    tiles["yt", g, h, i] = (y_units, P * i - cols.start)
+            nc.vector.scalar_tensor_tensor(
+                out=tiles["yt", g, h, cols.start // P][0][:, t, :],
+                in0=tiles["acc", g, h, 1, t, cols.start][:, : cols.stop - cols.start],
+                scalar=tiles["bias", 1][:, g, t : t + 1],
+                in1=tiles["piece", g, h, t][:, cols],
+                op0=ALU.add,
+                op1=ALU.max,
+            )
+
+        def turn_y(g, h, i):
+            bank = psum.tile([P, PACK, P], F32, name="turn", bufs=3)
+            y_units, offset = tiles["yt", g, h, i]
+            for t in range(PACK):
+                nc.tensor.transpose(bank[:, t, :], y_units[:, t, offset : offset + P], ident[:])
+            tiles["ybank", g, h, i] = bank
+
+        def store_y(g, h, i, engine):
+            rows = work.tile([P, P, PACK], F32, name="y_rows", bufs=6)
+            copy_on(engine, rows[:], tiles["ybank", g, h, i][:].rearrange("p t m -> p m t"))
+            first = SPAN * h + P * i
+            nc.sync.dma_start(
+                out=out_0[first : first + P, SPAN * g : SPAN * (g + 1)], in_=rows[:].rearrange("p m t -> p (m t)")
+            )
+
+        def round_y(g, h, engine, cols=slice(0, SPAN)):
+            grouped = work.tile([P, PACK * (cols.stop - cols.start)], BF16, name="y_grouped", bufs=3, align_bytes=64)
+            out = grouped[:].rearrange("p (c i t) -> p c t i", i=4, t=PACK)
+            in_ = tiles["yt", g, h, cols.start // P][0][:].rearrange("p t (c i) -> p c t i", i=4)
+            copy_on(engine, out, in_)
+            tiles["ygrp", g, h, cols.start] = grouped
+
+        def quant_y(g, h, cols=slice(0, SPAN)):
+            if h == 0 and cols.start == 0:
+                tiles["yq", g] = keep.tile([P, T], U32, name="y_codes_%d" % g, align_bytes=64)
+                tiles["ys", g] = keep.tile([P, T], U8, name="y_mxscales_%d" % g, align_bytes=64)
+            tokens = slice(SPAN * h + cols.start, SPAN * h + cols.stop)
+            source = tiles["ygrp", g, h, cols.start][:]
+            quantize(source, tiles["yq", g][:, tokens], tiles["ys", g][:, tokens])
+            words = out_1[g].rearrange("p m t -> p (m t)").bitcast(I32)
+            nc.sync.dma_start(out=words[:, tokens], in_=tiles["yq", g][:, tokens].bitcast(I32))
+            if tokens.stop == T:
+                for q in range(4):
+                    nc.sync.dma_start(
+                        out=out_2[g, 4 * q : 4 * q + 4, :].bitcast(I32),
+                        in_=tiles["ys", g][32 * q : 32 * q + 4, :].bitcast(I32),
+                    )
+
+        ident = keep.tile([P, P], F32, name="ident")
+        make_identity(nc, ident[:])
+
+        load_scales()
+        load_x(0, 0)
+        load_w(0, 0, 0)
+        load_x(0, 1)
+        load_w(0, 0, 1)
+        load_w(0, 0, 2)
+        load_bias(0)
+        load_bias(1)
+        for c in range(PASSES):
+            load_w(0, 1, c)
+        load_x(1, 0)
+        load_x(1, 1)
+        for w in range(2):
+            for c in range(PASSES):
+                load_w(1, w, c)
+
+        low, high = slice(0, 2 * P), slice(2 * P, SPAN)
+
+        def finish_rows(g, h, engines="SSSS", which=range(4)):
+            for i in which:
+                turn_y(g, h, i)
+                store_y(g, h, i, engines[i])
+
+        widen(0, [(0, 0), (0, 1), (1, 0), (1, 1)])
+        turn_x(0, 0, 0)
+        turn_x(0, 1, 0)
+        mix_w(0, 0, 0, "V")
+        copy_x(0, 0, 0, "S")
+        copy_x(0, 1, 0, "S")
+        widen(0, [(0, 2), (0, 3), (1, 2), (1, 3)])
+        turn_x(0, 0, 1)
+        turn_x(0, 1, 1)
+        mix_w(0, 0, 1, "S", 0, 32)
+        quant_w(0, 0, 0)
+        copy_x(0, 0, 1, "S")
+        copy_x(0, 1, 1, "S")
+        widen(0, [(2, i) for i in range(4)])
+        quant_x(0, 0)
+        turn_x(0, 2, 0)
+        turn_x(0, 2, 1)
+        one_pass(0, 0, 0, 0, 0)
+        mix_w(0, 0, 1, "S", 32, 64)
+        quant_x(0, 1)
+        mix_w(0, 0, 2, "V", 0, 32)
+        copy_x(0, 2, 0, "S")
+        copy_x(0, 2, 1, "S")
+        quant_w(0, 0, 1)
+        one_pass(0, 0, 0, 1, 1)
+        mix_w(0, 0, 2, "S", 32, 64)
+        mix_w(0, 1, 0, "V")
+        quant_x(0, 2)
+        quant_w(0, 0, 2)
+        one_pass(0, 0, 0, 2, 2)
+        mix_w(0, 1, 1, "S")
+        quant_w(0, 1, 0)
+        mix_w(0, 1, 2, "V")
+        for t in range(PACK):
+            first_piece(0, 0, t)
+        quant_w(0, 1, 1)
+        one_pass(0, 0, 1, 0, 0)
+        one_pass(0, 0, 1, 1, 1)
+        widen(1, [(0, 0), (0, 1), (1, 0)])
+        quant_w(0, 1, 2)
+        widen(1, [(1, 1), (2, 0), (2, 1)])
+        turn_x(1, 0, 0)
+        one_pass(0, 0, 1, 2, 2)
+        mix_w(1, 0, 0, "S", 0, 32)
+        copy_x(1, 0, 0, "S")
+        for c in (1, 2):
+            turn_x(1, c, 0)
+            copy_x(1, c, 0, "S")
+        mix_w(1, 0, 0, "S", 32, 64)
+        for t in range(PACK):
+            maxout(0, 0, t)
+            if t < 3:
+                quant_x(1, t, 0, 1)
+        widen(1, [(0, 2), (0, 3), (1, 2)])
+        widen(1, [(1, 3), (2, 2), (2, 3)])
+        mix_w(1, 0, 1, "S", 0, 32)
+        for t in range(PACK):
+            product(0, 1, 0, t, low)
+            first_piece(0, 1, t, low)
+        for c in range(PASSES):
+            turn_x(1, c, 1)
+            copy_x(1, c, 1, "S")
+        mix_w(1, 0, 2, "V")
+        mix_w(1, 0, 1, "S", 32, 64)
+        for t in range(PACK):
+            product(0, 1, 1, t, low)
+            maxout(0, 1, t, low)
+            if t < 3:
+                quant_x(1, t, 1, 1)
+        finish_rows(0, 0, "SSSS", (0, 1))
+        for c in (0, 2, 1):
+            quant_w(1, 0, c)
+        for t in range(PACK):
+            product(0, 1, 0, t, high)
+            first_piece(0, 1, t, high)
+        mix_w(1, 1, 0, "S", 0, 32)
+        mix_w(1, 1, 1, "V")
+        for t in range(PACK):
+            product(0, 1, 1, t, high)
+            maxout(0, 1, t, high)
+        finish_rows(0, 0, "SSSS", (2, 3))
+        mix_w(1, 1, 0, "S", 32, 64)
+        mix_w(1, 1, 2, "V")
+        for t in range(PACK):
+            product(1, 0, 0, t)
+            first_piece(1, 0, t)
+        for c in (1, 0, 2):
+            quant_w(1, 1, c)
+        round_y(0, 0, "V")
+        for t in range(PACK):
+            product(1, 0, 1, t)
+            maxout(1, 0, t)
+            if t == 0:
+                quant_y(0, 0)
+        third, last = slice(2 * P, 3 * P), slice(3 * P, SPAN)
+        finish_rows(0, 1)
+        round_y(0, 1, "V", low)
+        round_y(0, 1, "V", high)
+        for t in range(PACK):
+            product(1, 1, 0, t, low)
+            first_piece(1, 1, t, low)
+        quant_y(0, 1, low)
+        quant_y(0, 1, high)
+        round_y(1, 0, "V")
+        finish_rows(1, 0, "SSSS", (0, 1))
+        for t in range(PACK):
+            product(1, 1, 1, t, low)
+            maxout(1, 1, t, low)
+        finish_rows(1, 0, "SSSS", (2, 3))
+        for t in range(PACK):
+            product(1, 1, 0, t, third)
+            first_piece(1, 1, t, third)
+        quant_y(1, 0)
+        round_y(1, 1, "V", low)
+        for t in range(PACK):
+            product(1, 1, 1, t, third)
+            maxout(1, 1, t, third)
+        finish_rows(1, 1, "SSSS", (0, 1))
+        quant_y(1, 1, low)
+        round_y(1, 1, "V", third)
+        for t in range(PACK):
+            product(1, 1, 0, t, last)
+            first_piece(1, 1, t, last)
+        finish_rows(1, 1, "SSSS", (2,))
+        for t in range(PACK):
+            product(1, 1, 1, t, last)
+            maxout(1, 1, t, last)
+            if t == 0:
+                quant_y(1, 1, third)
+        round_y(1, 1, "V", last)
+        finish_rows(1, 1, "SSSS", (3,))
+        quant_y(1, 1, last)

@@ -35,6 +35,9 @@ def tile_maxout_patch_layer_b1_kernel(tc, X_bytes, X_scale, W1, W2, b1, b2, out_
         ctx.enter_context(tc.manual_schedule())
 
         tiles = {}
+        x_banks = [5 + n % 3 for n in range(12)]
+        sum_banks = [0, 1, 2, 3, 4, 0, 1, 2, 3, 5, 6, 7] + [(4 + n) % 6 for n in range(40)]
+        y_banks = [6 + n % 2 for n in range(16)]
 
         def copy_on(engine, out, in_):
             if engine == "V":
@@ -43,14 +46,14 @@ def tile_maxout_patch_layer_b1_kernel(tc, X_bytes, X_scale, W1, W2, b1, b2, out_
                 nc.scalar.copy(out=out, in_=in_)
 
         def load_scales():
-            xs = keep.tile([P, T // P, BLOCKS], F32, name="x_scale")
-            nc.sync.dma_start(out=xs[:], in_=X_scale.rearrange("(i p) j -> p i j", p=P))
+            xs = keep.tile([P, T // (2 * P), 2 * BLOCKS], F32, name="x_scale")
+            nc.sync.dma_start(out=xs[:], in_=X_scale.rearrange("(d p i) j -> p d (i j)", p=P, i=2))
             tiles["xs"] = xs
 
         def load_x(h, b):
-            xb = keep.tile([P, 2, K], U8, name="x_bytes_%d_%d" % (h, b))
+            xb = keep.tile([P, 2 * K], U8, name="x_bytes_%d_%d" % (h, b))
             first = SPAN * h + 2 * P * b
-            nc.sync.dma_start(out=xb[:], in_=X_bytes[first : first + 2 * P, :].rearrange("(i p) k -> p i k", p=P))
+            nc.sync.dma_start(out=xb[:], in_=X_bytes[first : first + 2 * P, :].rearrange("(p i) k -> p (i k)", i=2))
             tiles["xb", h, b] = xb
 
         def load_w(g, w, c):
@@ -60,41 +63,39 @@ def tile_maxout_patch_layer_b1_kernel(tc, X_bytes, X_scale, W1, W2, b1, b2, out_
             tiles["wraw", g, w, c] = raw
 
         def load_bias(w):
-            raw = keep.tile([P, N // SPAN, PACK], BF16, name="bias_raw_%d" % w)
-            nc.sync.dma_start(out=raw[:], in_=biases[w].rearrange("(g p t) -> p g t", p=P, t=PACK))
+            raw = keep.tile([P, N // SPAN, 16], BF16, name="bias_raw_%d" % w)
+            nc.sync.dma_start(out=raw[:, :, :PACK], in_=biases[w].rearrange("(g p t) -> p g t", p=P, t=PACK))
             bias = keep.tile([P, N // SPAN, PACK], F32, name="bias_%d" % w)
-            nc.gpsimd.tensor_copy(out=bias[:], in_=raw[:])
+            nc.gpsimd.tensor_copy(out=bias[:], in_=raw[:, :, :PACK])
             tiles["bias", w] = bias
 
-        def widen(h, jobs):
-            for c, i in jobs:
-                tiles["wide", h, c, i] = work.tile([P, SPAN], BF16, name="x_wide", bufs=8)
-            for q in range(4):
-                for c, i in jobs:
+        def widen(h, c, b, engine):
+            wide = work.tile([P, 2, SPAN], BF16, name="x_wide", bufs=6)
+            for i in range(2):
+                for q in range(4):
                     j = 4 * c + q
-                    codes = tiles["xb", h, i // 2][:, i % 2, P * j : P * (j + 1)].bitcast(FP8)
-                    halves = tiles["wide", h, c, i][:].rearrange("p (u q r e) -> p q r u e", u=2, q=4, e=2)
-                    nc.vector.tensor_scalar(
-                        out=halves[:, q],
-                        in0=codes.rearrange("p (r u e) -> p r u e", u=2, e=2),
-                        scalar1=tiles["xs"][:, 4 * h + i, j : j + 1],
-                        scalar2=None,
-                        op0=ALU.mult,
-                    )
+                    codes = tiles["xb", h, b][:, K * i + P * j : K * i + P * (j + 1)].bitcast(FP8)
+                    scale = tiles["xs"][:, 2 * h + b, BLOCKS * i + j : BLOCKS * i + j + 1]
+                    out = wide[:, i, P * q : P * (q + 1)]
+                    if engine == "V":
+                        nc.vector.tensor_scalar(out=out, in0=codes, scalar1=scale, scalar2=None, op0=ALU.mult)
+                    else:
+                        nc.scalar.activation(out=out, in_=codes, func=ACT.Copy, scale=scale)
+            tiles["wide", h, c, b] = wide
 
         def turn_x(h, c, b):
-            bank = psum.tile([P, 2, 2, P], F32, name="turn", bufs=3)
+            bank = psum.tile([P, 2, 2, P], F32, name="bank_%d" % x_banks.pop(0))
             for i in range(2):
-                words = tiles["wide", h, c, 2 * b + i][:].bitcast(F32)
+                words = tiles["wide", h, c, b][:, i, :].bitcast(F32)
                 for u in range(2):
-                    nc.tensor.transpose(bank[:, i, u, :], words[:, P * u : P * (u + 1)], ident[:])
+                    nc.tensor.transpose(bank[:, i, u, :], words[:, u : 2 * P : 2], ident[:])
             tiles["xbank", h, c, b] = bank
 
         def copy_x(h, c, b, engine):
             if b == 0:
                 tiles["xgrp", h, c] = work.tile([P, 2, 2 * P * PACK], BF16, name="x_grouped", bufs=3, align_bytes=64)
-            words = tiles["xgrp", h, c][:, b, :].bitcast(F32).rearrange("p (i r u) -> p i r u", i=2, u=2)
-            copy_on(engine, words, tiles["xbank", h, c, b][:].rearrange("p i u r -> p i r u"))
+            words = tiles["xgrp", h, c][:, b, :].bitcast(F32).rearrange("p (r i u) -> p r i u", i=2, u=2)
+            copy_on(engine, words, tiles["xbank", h, c, b][:].rearrange("p i u r -> p r i u"))
 
         def quantize(source, codes, scales):
             nc.vector.quantize_mx(out=codes.bitcast(FP8X4), scales=scales, in_=source)
@@ -125,7 +126,7 @@ def tile_maxout_patch_layer_b1_kernel(tc, X_bytes, X_scale, W1, W2, b1, b2, out_
         def multiply(g, h, w, t, c, step, cols=slice(0, SPAN)):
             key = ("acc", g, h, w, t, cols.start)
             if step == 0:
-                tiles[key] = psum.tile([P, SPAN], F32, name="acc", bufs=5)
+                tiles[key] = psum.tile([P, SPAN], F32, name="bank_%d" % sum_banks.pop(0))
             w_codes, w_scales = tiles["wq", g, w, c]
             x_codes, x_scales = tiles["xq", h, c]
             units = slice(P * t, P * (t + 1))
@@ -173,7 +174,7 @@ def tile_maxout_patch_layer_b1_kernel(tc, X_bytes, X_scale, W1, W2, b1, b2, out_
             )
 
         def turn_y(g, h, i):
-            bank = psum.tile([P, PACK, P], F32, name="turn", bufs=3)
+            bank = psum.tile([P, PACK, P], F32, name="bank_%d" % y_banks.pop(0))
             y_units, offset = tiles["yt", g, h, i]
             for t in range(PACK):
                 nc.tensor.transpose(bank[:, t, :], y_units[:, t, offset : offset + P], ident[:])
@@ -189,8 +190,8 @@ def tile_maxout_patch_layer_b1_kernel(tc, X_bytes, X_scale, W1, W2, b1, b2, out_
 
         def round_y(g, h, engine, cols=slice(0, SPAN)):
             grouped = work.tile([P, PACK * (cols.stop - cols.start)], BF16, name="y_grouped", bufs=3, align_bytes=64)
-            out = grouped[:].rearrange("p (c i t) -> p c t i", i=4, t=PACK)
-            in_ = tiles["yt", g, h, cols.start // P][0][:].rearrange("p t (c i) -> p c t i", i=4)
+            out = grouped[:].rearrange("p (c i t) -> p c i t", i=4, t=PACK)
+            in_ = tiles["yt", g, h, cols.start // P][0][:].rearrange("p t (c i) -> p c i t", i=4)
             copy_on(engine, out, in_)
             tiles["ygrp", g, h, cols.start] = grouped
 
@@ -213,158 +214,138 @@ def tile_maxout_patch_layer_b1_kernel(tc, X_bytes, X_scale, W1, W2, b1, b2, out_
         ident = keep.tile([P, P], F32, name="ident")
         make_identity(nc, ident[:])
 
-        load_scales()
         load_x(0, 0)
+        load_scales()
         load_w(0, 0, 0)
         load_x(0, 1)
         load_w(0, 0, 1)
         load_w(0, 0, 2)
-        load_bias(0)
-        load_bias(1)
-        for c in range(PASSES):
-            load_w(0, 1, c)
         load_x(1, 0)
         load_x(1, 1)
+        load_bias(0)
+        for c in range(PASSES):
+            load_w(0, 1, c)
+        load_bias(1)
         for w in range(2):
             for c in range(PASSES):
                 load_w(1, w, c)
 
         low, high = slice(0, 2 * P), slice(2 * P, SPAN)
+        third, last = slice(2 * P, 3 * P), slice(3 * P, SPAN)
 
         def finish_rows(g, h, engines="SSSS", which=range(4)):
             for i in which:
                 turn_y(g, h, i)
                 store_y(g, h, i, engines[i])
 
-        widen(0, [(0, 0), (0, 1), (1, 0), (1, 1)])
-        turn_x(0, 0, 0)
-        turn_x(0, 1, 0)
+        widen(0, 0, 0, "V")
+        widen(0, 1, 0, "S")
+        widen(0, 2, 0, "V")
+        for c in range(PASSES):
+            turn_x(0, c, 0)
+            copy_x(0, c, 0, "S")
         mix_w(0, 0, 0, "V")
-        copy_x(0, 0, 0, "S")
-        copy_x(0, 1, 0, "S")
-        widen(0, [(0, 2), (0, 3), (1, 2), (1, 3)])
-        turn_x(0, 0, 1)
-        turn_x(0, 1, 1)
         mix_w(0, 0, 1, "S", 0, 32)
-        quant_w(0, 0, 0)
-        copy_x(0, 0, 1, "S")
-        copy_x(0, 1, 1, "S")
-        widen(0, [(2, i) for i in range(4)])
+        for c in range(PASSES):
+            widen(0, c, 1, "V")
+            turn_x(0, c, 1)
+            copy_x(0, c, 1, "S")
+            if c == 1:
+                quant_w(0, 0, 0)
         quant_x(0, 0)
-        turn_x(0, 2, 0)
-        turn_x(0, 2, 1)
         one_pass(0, 0, 0, 0, 0)
         mix_w(0, 0, 1, "S", 32, 64)
         quant_x(0, 1)
         mix_w(0, 0, 2, "V", 0, 32)
-        copy_x(0, 2, 0, "S")
-        copy_x(0, 2, 1, "S")
+        mix_w(0, 0, 2, "S", 32, 64)
+        quant_x(0, 2)
         quant_w(0, 0, 1)
         one_pass(0, 0, 0, 1, 1)
-        mix_w(0, 0, 2, "S", 32, 64)
-        mix_w(0, 1, 0, "V")
-        quant_x(0, 2)
+        for b in range(2):
+            widen(1, 0, b, "V")
+            turn_x(1, 0, b)
         quant_w(0, 0, 2)
         one_pass(0, 0, 0, 2, 2)
+        mix_w(0, 1, 0, "S", 0, 32)
+        for b in range(2):
+            copy_x(1, 0, b, "S")
+            widen(1, 1, b, "V")
+            turn_x(1, 1, b)
+        quant_x(1, 0)
+        first_piece(0, 0, 0)
+        widen(1, 2, 0, "V")
+        widen(1, 2, 1, "V")
+        copy_x(1, 1, 0, "S")
+        first_piece(0, 0, 1)
+        copy_x(1, 1, 1, "S")
+        first_piece(0, 0, 2)
+        first_piece(0, 0, 3)
+        turn_x(1, 2, 0)
+        turn_x(1, 2, 1)
+        one_pass(0, 1, 0, 0, 0)
+        copy_x(1, 2, 0, "V")
+        copy_x(1, 2, 1, "V")
+        quant_x(1, 1)
+        quant_x(1, 2)
+        one_pass(0, 1, 0, 1, 1)
+        one_pass(0, 1, 0, 2, 2)
         mix_w(0, 1, 1, "S")
-        quant_w(0, 1, 0)
+        mix_w(0, 1, 0, "V", 32, 64)
         mix_w(0, 1, 2, "V")
         for t in range(PACK):
-            first_piece(0, 0, t)
-        quant_w(0, 1, 1)
-        one_pass(0, 0, 1, 0, 0)
-        one_pass(0, 0, 1, 1, 1)
-        widen(1, [(0, 0), (0, 1), (1, 0)])
-        quant_w(0, 1, 2)
-        widen(1, [(1, 1), (2, 0), (2, 1)])
-        turn_x(1, 0, 0)
-        one_pass(0, 0, 1, 2, 2)
-        mix_w(1, 0, 0, "S", 0, 32)
-        copy_x(1, 0, 0, "S")
-        for c in (1, 2):
-            turn_x(1, c, 0)
-            copy_x(1, c, 0, "S")
-        mix_w(1, 0, 0, "S", 32, 64)
+            first_piece(0, 1, t)
+        for step, c in enumerate((0, 2, 1)):
+            quant_w(0, 1, c)
+            one_pass(0, 0, 1, c, step)
+        mix_w(1, 0, 0, "V")
+        mix_w(1, 0, 1, "S")
         for t in range(PACK):
             maxout(0, 0, t)
-            if t < 3:
-                quant_x(1, t, 0, 1)
-        widen(1, [(0, 2), (0, 3), (1, 2)])
-        widen(1, [(1, 3), (2, 2), (2, 3)])
-        mix_w(1, 0, 1, "S", 0, 32)
+        quant_w(1, 0, 0)
+        mix_w(1, 0, 2, "S")
+        quant_w(1, 0, 1)
         for t in range(PACK):
-            product(0, 1, 0, t, low)
-            first_piece(0, 1, t, low)
-        for c in range(PASSES):
-            turn_x(1, c, 1)
-            copy_x(1, c, 1, "S")
-        mix_w(1, 0, 2, "V")
-        mix_w(1, 0, 1, "S", 32, 64)
-        for t in range(PACK):
-            product(0, 1, 1, t, low)
-            maxout(0, 1, t, low)
-            if t < 3:
-                quant_x(1, t, 1, 1)
+            product(0, 1, 1, t)
+            maxout(0, 1, t)
+            if t == 1:
+                quant_w(1, 0, 2)
         finish_rows(0, 0, "SSSS", (0, 1))
-        for c in (0, 2, 1):
-            quant_w(1, 0, c)
-        for t in range(PACK):
-            product(0, 1, 0, t, high)
-            first_piece(0, 1, t, high)
-        mix_w(1, 1, 0, "S", 0, 32)
+        mix_w(1, 1, 0, "V")
         mix_w(1, 1, 1, "V")
-        for t in range(PACK):
-            product(0, 1, 1, t, high)
-            maxout(0, 1, t, high)
-        finish_rows(0, 0, "SSSS", (2, 3))
-        mix_w(1, 1, 0, "S", 32, 64)
-        mix_w(1, 1, 2, "V")
         for t in range(PACK):
             product(1, 0, 0, t)
             first_piece(1, 0, t)
-        for c in (1, 0, 2):
-            quant_w(1, 1, c)
+        quant_w(1, 1, 0)
+        mix_w(1, 1, 2, "V")
+        quant_w(1, 1, 1)
+        finish_rows(0, 0, "SSSS", (2, 3))
         round_y(0, 0, "V")
+        quant_w(1, 1, 2)
+        for t in range(PACK):
+            product(1, 1, 0, t)
+            first_piece(1, 1, t)
+        quant_y(0, 0)
+        round_y(0, 1, "V")
+        finish_rows(0, 1, "SSSS", (0, 1))
         for t in range(PACK):
             product(1, 0, 1, t)
             maxout(1, 0, t)
             if t == 0:
-                quant_y(0, 0)
-        third, last = slice(2 * P, 3 * P), slice(3 * P, SPAN)
-        finish_rows(0, 1)
-        round_y(0, 1, "V", low)
-        round_y(0, 1, "V", high)
-        for t in range(PACK):
-            product(1, 1, 0, t, low)
-            first_piece(1, 1, t, low)
-        quant_y(0, 1, low)
-        quant_y(0, 1, high)
+                quant_y(0, 1)
+        finish_rows(0, 1, "SSSS", (2, 3))
         round_y(1, 0, "V")
-        finish_rows(1, 0, "SSSS", (0, 1))
         for t in range(PACK):
             product(1, 1, 1, t, low)
             maxout(1, 1, t, low)
-        finish_rows(1, 0, "SSSS", (2, 3))
-        for t in range(PACK):
-            product(1, 1, 0, t, third)
-            first_piece(1, 1, t, third)
         quant_y(1, 0)
+        finish_rows(1, 0, "SSSS")
         round_y(1, 1, "V", low)
         for t in range(PACK):
-            product(1, 1, 1, t, third)
-            maxout(1, 1, t, third)
-        finish_rows(1, 1, "SSSS", (0, 1))
-        quant_y(1, 1, low)
-        round_y(1, 1, "V", third)
-        for t in range(PACK):
-            product(1, 1, 0, t, last)
-            first_piece(1, 1, t, last)
-        finish_rows(1, 1, "SSSS", (2,))
-        for t in range(PACK):
-            product(1, 1, 1, t, last)
-            maxout(1, 1, t, last)
+            product(1, 1, 1, t, high)
+            maxout(1, 1, t, high)
             if t == 0:
-                quant_y(1, 1, third)
-        round_y(1, 1, "V", last)
-        finish_rows(1, 1, "SSSS", (3,))
-        quant_y(1, 1, last)
+                quant_y(1, 1, low)
+        finish_rows(1, 1, "SSSS", (0, 1))
+        round_y(1, 1, "V", high)
+        finish_rows(1, 1, "SSSV", (2, 3))
+        quant_y(1, 1, high)

@@ -36,8 +36,8 @@ def tile_maxout_patch_layer_b1_kernel(tc, X_bytes, X_scale, W1, W2, b1, b2, out_
 
         tiles = {}
         x_banks = [5 + n % 3 for n in range(12)]
-        sum_banks = [0, 1, 2, 3, 4, 0, 1, 2, 3, 5, 6, 7] + [(4 + n) % 6 for n in range(40)]
-        y_banks = [6 + n % 2 for n in range(16)]
+        sum_banks = [0, 1, 2, 3, 4, 0, 1, 2, 3, 5, 6, 7] + [4, 5, 0, 1, 2, 3, 4, 5] + [0, 1, 2, 3] + [4, 5, 0, 1] + [4, 5, 0, 1] + [2, 3, 4, 5]
+        y_banks = [6, 7] * 4 + [2, 3, 6, 7] + [0, 1, 6, 7]
 
         def copy_on(engine, out, in_):
             if engine == "V":
@@ -47,7 +47,7 @@ def tile_maxout_patch_layer_b1_kernel(tc, X_bytes, X_scale, W1, W2, b1, b2, out_
 
         def load_scales():
             xs = keep.tile([P, T // (2 * P), 2 * BLOCKS], F32, name="x_scale")
-            nc.sync.dma_start(out=xs[:], in_=X_scale.rearrange("(d p i) j -> p d (i j)", p=P, i=2))
+            nc.scalar.dma_start(out=xs[:], in_=X_scale.rearrange("(d p i) j -> p d (i j)", p=P, i=2))
             tiles["xs"] = xs
 
         def load_x(h, b):
@@ -65,9 +65,7 @@ def tile_maxout_patch_layer_b1_kernel(tc, X_bytes, X_scale, W1, W2, b1, b2, out_
         def load_bias(w):
             raw = keep.tile([P, N // SPAN, 16], BF16, name="bias_raw_%d" % w)
             nc.sync.dma_start(out=raw[:, :, :PACK], in_=biases[w].rearrange("(g p t) -> p g t", p=P, t=PACK))
-            bias = keep.tile([P, N // SPAN, PACK], F32, name="bias_%d" % w)
-            nc.gpsimd.tensor_copy(out=bias[:], in_=raw[:, :, :PACK])
-            tiles["bias", w] = bias
+            tiles["bias", w] = raw
 
         def widen(h, c, b, engine):
             wide = work.tile([P, 2, SPAN], BF16, name="x_wide", bufs=6)
@@ -204,18 +202,26 @@ def tile_maxout_patch_layer_b1_kernel(tc, X_bytes, X_scale, W1, W2, b1, b2, out_
             quantize(source, tiles["yq", g][:, tokens], tiles["ys", g][:, tokens])
             words = out_1[g].rearrange("p m t -> p (m t)").bitcast(I32)
             nc.sync.dma_start(out=words[:, tokens], in_=tiles["yq", g][:, tokens].bitcast(I32))
-            if tokens.stop == T:
-                for q in range(4):
-                    nc.sync.dma_start(
-                        out=out_2[g, 4 * q : 4 * q + 4, :].bitcast(I32),
-                        in_=tiles["ys", g][32 * q : 32 * q + 4, :].bitcast(I32),
-                    )
 
+        def store_scales(g):
+            for q in range(4):
+                nc.sync.dma_start(
+                    out=out_2[g, 4 * q : 4 * q + 4, :].bitcast(I32),
+                    in_=tiles["ys", g][32 * q : 32 * q + 4, :].bitcast(I32),
+                )
+
+        def keep_warm(count):
+            for step in range(count):
+                nc.tensor.matmul(out=idle_bank[:], lhsT=zeros[:, :P], rhs=zeros[:], start=True, stop=True)
+
+        zeros = keep.tile([P, SPAN], BF16, name="zeros")
+        nc.vector.memset(zeros[:], 0.0)
+        idle_bank = psum.tile([P, SPAN], F32, name="bank_4")
         ident = keep.tile([P, P], F32, name="ident")
         make_identity(nc, ident[:])
 
-        load_x(0, 0)
         load_scales()
+        load_x(0, 0)
         load_w(0, 0, 0)
         load_x(0, 1)
         load_w(0, 0, 1)
@@ -241,13 +247,17 @@ def tile_maxout_patch_layer_b1_kernel(tc, X_bytes, X_scale, W1, W2, b1, b2, out_
         widen(0, 0, 0, "V")
         widen(0, 1, 0, "S")
         widen(0, 2, 0, "V")
+        keep_warm(6)
         for c in range(PASSES):
             turn_x(0, c, 0)
             copy_x(0, c, 0, "S")
+        keep_warm(3)
         mix_w(0, 0, 0, "V")
         mix_w(0, 0, 1, "S", 0, 32)
         for c in range(PASSES):
             widen(0, c, 1, "V")
+            if c == 2:
+                keep_warm(2)
             turn_x(0, c, 1)
             copy_x(0, c, 1, "S")
             if c == 1:
@@ -266,86 +276,101 @@ def tile_maxout_patch_layer_b1_kernel(tc, X_bytes, X_scale, W1, W2, b1, b2, out_
             turn_x(1, 0, b)
         quant_w(0, 0, 2)
         one_pass(0, 0, 0, 2, 2)
-        mix_w(0, 1, 0, "S", 0, 32)
+        mix_w(0, 1, 0, "S")
         for b in range(2):
             copy_x(1, 0, b, "S")
             widen(1, 1, b, "V")
             turn_x(1, 1, b)
-        quant_x(1, 0)
-        first_piece(0, 0, 0)
         widen(1, 2, 0, "V")
         widen(1, 2, 1, "V")
-        copy_x(1, 1, 0, "S")
-        first_piece(0, 0, 1)
-        copy_x(1, 1, 1, "S")
-        first_piece(0, 0, 2)
-        first_piece(0, 0, 3)
         turn_x(1, 2, 0)
-        turn_x(1, 2, 1)
+        quant_x(1, 0)
+        for t in range(PACK):
+            first_piece(0, 0, t)
+        copy_x(1, 1, 0, "V")
+        copy_x(1, 1, 1, "V")
         one_pass(0, 1, 0, 0, 0)
-        copy_x(1, 2, 0, "V")
-        copy_x(1, 2, 1, "V")
+        turn_x(1, 2, 1)
+        copy_x(1, 2, 0, "S")
+        mix_w(0, 1, 1, "S", 0, 32)
+        copy_x(1, 2, 1, "S")
+        quant_w(0, 1, 0)
         quant_x(1, 1)
-        quant_x(1, 2)
         one_pass(0, 1, 0, 1, 1)
-        one_pass(0, 1, 0, 2, 2)
-        mix_w(0, 1, 1, "S")
-        mix_w(0, 1, 0, "V", 32, 64)
+        mix_w(0, 1, 1, "S", 32, 64)
+        one_pass(0, 0, 1, 0, 0)
         mix_w(0, 1, 2, "V")
+        quant_x(1, 2)
+        one_pass(0, 1, 0, 2, 2)
         for t in range(PACK):
             first_piece(0, 1, t)
-        for step, c in enumerate((0, 2, 1)):
+        for step, c in ((1, 2), (2, 1)):
             quant_w(0, 1, c)
             one_pass(0, 0, 1, c, step)
         mix_w(1, 0, 0, "V")
+        mix_w(1, 0, 2, "V", 0, 32)
         mix_w(1, 0, 1, "S")
         for t in range(PACK):
             maxout(0, 0, t)
         quant_w(1, 0, 0)
-        mix_w(1, 0, 2, "S")
+        mix_w(1, 0, 2, "S", 32, 64)
         quant_w(1, 0, 1)
         for t in range(PACK):
             product(0, 1, 1, t)
             maxout(0, 1, t)
             if t == 1:
                 quant_w(1, 0, 2)
+        mix_w(1, 1, 0, "S")
         finish_rows(0, 0, "SSSS", (0, 1))
-        mix_w(1, 1, 0, "V")
         mix_w(1, 1, 1, "V")
+        quant_w(1, 1, 0)
+        mix_w(1, 1, 2, "V")
         for t in range(PACK):
             product(1, 0, 0, t)
             first_piece(1, 0, t)
-        quant_w(1, 1, 0)
-        mix_w(1, 1, 2, "V")
-        quant_w(1, 1, 1)
         finish_rows(0, 0, "SSSS", (2, 3))
+        for c in range(PASSES):
+            if c > 0:
+                quant_w(1, 1, c)
+            one_pass(1, 0, 1, c, c)
         round_y(0, 0, "V")
-        quant_w(1, 1, 2)
+        finish_rows(0, 1, "SSSS", (0, 1))
+        for t in range(PACK):
+            maxout(1, 0, t)
+            if t == 0:
+                quant_y(0, 0)
+        round_y(0, 1, "V")
         for t in range(PACK):
             product(1, 1, 0, t)
             first_piece(1, 1, t)
-        quant_y(0, 0)
-        round_y(0, 1, "V")
-        finish_rows(0, 1, "SSSS", (0, 1))
-        for t in range(PACK):
-            product(1, 0, 1, t)
-            maxout(1, 0, t)
-            if t == 0:
-                quant_y(0, 1)
-        finish_rows(0, 1, "SSSS", (2, 3))
         round_y(1, 0, "V")
+        quant_y(0, 1)
+        turn_y(0, 1, 2)
+        turn_y(0, 1, 3)
+        turn_y(1, 0, 0)
+        turn_y(1, 0, 1)
+        store_y(0, 1, 2, "S")
+        store_y(0, 1, 3, "S")
+        store_y(1, 0, 0, "S")
+        store_y(1, 0, 1, "S")
+        store_scales(0)
+        quant_y(1, 0)
         for t in range(PACK):
             product(1, 1, 1, t, low)
             maxout(1, 1, t, low)
-        quant_y(1, 0)
-        finish_rows(1, 0, "SSSS")
+        finish_rows(1, 0, "SSSS", (2, 3))
         round_y(1, 1, "V", low)
         for t in range(PACK):
             product(1, 1, 1, t, high)
-            maxout(1, 1, t, high)
             if t == 0:
                 quant_y(1, 1, low)
-        finish_rows(1, 1, "SSSS", (0, 1))
+            if t == 1:
+                finish_rows(1, 1, "SSSS", (0, 1))
+            maxout(1, 1, t, high)
         round_y(1, 1, "V", high)
-        finish_rows(1, 1, "SSSV", (2, 3))
+        turn_y(1, 1, 2)
+        turn_y(1, 1, 3)
+        store_y(1, 1, 2, "S")
         quant_y(1, 1, high)
+        store_y(1, 1, 3, "S")
+        store_scales(1)

@@ -19,8 +19,19 @@ ACT = mybir.ActivationFunctionType
 P = 128
 PACK = 4
 SPAN = P * PACK
+PAIR = 2 * P
 PASSES = K // SPAN
 BLOCKS = K // P
+BANKS = 8
+RUNS = SPAN // 8
+
+CUT_FIRST_W1, CUT_FIRST_W2, CUT_SECOND_W1 = 48, 16, 32
+
+WARM_FIRST, WARM_BETWEEN = 6, 2
+
+ALL = slice(0, SPAN)
+LOW, HIGH = slice(0, PAIR), slice(PAIR, SPAN)
+THIRD, LAST = slice(PAIR, 3 * P), slice(3 * P, SPAN)
 
 
 def tile_maxout_patch_layer_b1_kernel(tc, X_bytes, X_scale, W1, W2, b1, b2, out_0, out_1, out_2):
@@ -30,106 +41,123 @@ def tile_maxout_patch_layer_b1_kernel(tc, X_bytes, X_scale, W1, W2, b1, b2, out_
 
     with ExitStack() as ctx:
         keep = ctx.enter_context(tc.tile_pool(name="keep", bufs=1))
-        work = ctx.enter_context(tc.tile_pool(name="work", bufs=3))
+        work = ctx.enter_context(tc.tile_pool(name="work", bufs=1))
         psum = ctx.enter_context(tc.psum_pool(name="psum", bufs=1))
         ctx.enter_context(tc.manual_schedule())
 
         tiles = {}
-        x_banks = [5 + n % 3 for n in range(12)]
-        sum_banks = [0, 1, 2, 3, 4, 0, 1, 2, 3, 5, 6, 7] + [4, 5, 0, 1, 2, 3, 4, 5] + [0, 1, 2, 3] + [4, 5, 0, 1] + [4, 5, 0, 1] + [2, 3, 4, 5]
-        y_banks = [6, 7] * 4 + [2, 3, 6, 7] + [0, 1, 6, 7]
+        free_banks = list(range(BANKS))
+
+        def take_bank(key, shape):
+            number = free_banks.pop(0)
+            tiles[key] = psum.tile(shape, F32, name="bank_%d" % number)
+            tiles["bank of", key] = number
+            return tiles[key]
+
+        def free_bank(key):
+            free_banks.append(tiles["bank of", key])
 
         def copy_on(engine, out, in_):
-            if engine == "V":
+            if engine == "vector":
                 nc.vector.tensor_copy(out=out, in_=in_)
             else:
                 nc.scalar.copy(out=out, in_=in_)
 
-        def load_scales():
-            xs = keep.tile([P, T // (2 * P), 2 * BLOCKS], F32, name="x_scale")
-            nc.scalar.dma_start(out=xs[:], in_=X_scale.rearrange("(d p i) j -> p d (i j)", p=P, i=2))
-            tiles["xs"] = xs
-
-        def load_x(h, b):
-            xb = keep.tile([P, 2 * K], U8, name="x_bytes_%d_%d" % (h, b))
-            first = SPAN * h + 2 * P * b
-            nc.sync.dma_start(out=xb[:], in_=X_bytes[first : first + 2 * P, :].rearrange("(p i) k -> p (i k)", i=2))
-            tiles["xb", h, b] = xb
-
-        def load_w(g, w, c):
-            raw = keep.tile([P, PACK, SPAN], BF16, name="w_raw_%d_%d_%d" % (g, w, c))
-            rows = weights[w][SPAN * c : SPAN * (c + 1), SPAN * g : SPAN * (g + 1)]
-            nc.sync.dma_start(out=raw[:], in_=rows.rearrange("(p j) n -> p j n", j=PACK))
-            tiles["wraw", g, w, c] = raw
-
-        def load_bias(w):
-            raw = keep.tile([P, N // SPAN, 16], BF16, name="bias_raw_%d" % w)
-            nc.sync.dma_start(out=raw[:, :, :PACK], in_=biases[w].rearrange("(g p t) -> p g t", p=P, t=PACK))
-            tiles["bias", w] = raw
-
-        def widen(h, c, b, engine):
-            wide = work.tile([P, 2, SPAN], BF16, name="x_wide", bufs=6)
-            for i in range(2):
-                for q in range(4):
-                    j = 4 * c + q
-                    codes = tiles["xb", h, b][:, K * i + P * j : K * i + P * (j + 1)].bitcast(FP8)
-                    scale = tiles["xs"][:, 2 * h + b, BLOCKS * i + j : BLOCKS * i + j + 1]
-                    out = wide[:, i, P * q : P * (q + 1)]
-                    if engine == "V":
-                        nc.vector.tensor_scalar(out=out, in0=codes, scalar1=scale, scalar2=None, op0=ALU.mult)
-                    else:
-                        nc.scalar.activation(out=out, in_=codes, func=ACT.Copy, scale=scale)
-            tiles["wide", h, c, b] = wide
-
-        def turn_x(h, c, b):
-            bank = psum.tile([P, 2, 2, P], F32, name="bank_%d" % x_banks.pop(0))
-            for i in range(2):
-                words = tiles["wide", h, c, b][:, i, :].bitcast(F32)
-                for u in range(2):
-                    nc.tensor.transpose(bank[:, i, u, :], words[:, u : 2 * P : 2], ident[:])
-            tiles["xbank", h, c, b] = bank
-
-        def copy_x(h, c, b, engine):
-            if b == 0:
-                tiles["xgrp", h, c] = work.tile([P, 2, 2 * P * PACK], BF16, name="x_grouped", bufs=3, align_bytes=64)
-            words = tiles["xgrp", h, c][:, b, :].bitcast(F32).rearrange("p (r i u) -> p r i u", i=2, u=2)
-            copy_on(engine, words, tiles["xbank", h, c, b][:].rearrange("p i u r -> p r i u"))
-
         def quantize(source, codes, scales):
             nc.vector.quantize_mx(out=codes.bitcast(FP8X4), scales=scales, in_=source)
 
-        def quant_x(h, c, first=0, pairs=2):
+
+        def load_x_scales(first, count):
+            x_scale = keep.tile([P, count, 2 * BLOCKS], F32, name="x_scale_%d" % first)
+            rows = X_scale[PAIR * first : PAIR * (first + count), :]
+            nc.scalar.dma_start(out=x_scale[:], in_=rows.rearrange("(d p i) j -> p d (i j)", p=P, i=2))
+            for d in range(count):
+                tiles["x_scale", first + d] = x_scale[:, d, :]
+
+        def load_x(h, b, first=0, count=PASSES):
+            x_bytes = keep.tile([P, 2, SPAN * count], U8, name="x_bytes_%d_%d_%d" % (h, b, first))
+            patch = SPAN * h + PAIR * b
+            rows = X_bytes[patch : patch + PAIR, SPAN * first : SPAN * (first + count)]
+            nc.sync.dma_start(out=x_bytes[:], in_=rows.rearrange("(p i) k -> p i k", i=2))
+            for c in range(count):
+                tiles["x_bytes", h, b, first + c] = x_bytes[:, :, SPAN * c : SPAN * (c + 1)]
+
+        def load_w(g, w, c):
+            w_rows = keep.tile([P, PACK, SPAN], BF16, name="w_rows_%d_%d_%d" % (g, w, c))
+            rows = weights[w][SPAN * c : SPAN * (c + 1), SPAN * g : SPAN * (g + 1)]
+            nc.sync.dma_start(out=w_rows[:], in_=rows.rearrange("(p j) n -> p j n", j=PACK))
+            tiles["w_rows", g, w, c] = w_rows
+
+        def load_bias(w):
+            bias = keep.tile([P, N // SPAN, 16], BF16, name="bias_%d" % w)
+            nc.sync.dma_start(out=bias[:, :, :PACK], in_=biases[w].rearrange("(g p t) -> p g t", p=P, t=PACK))
+            tiles["bias", w] = bias
+
+
+        def widen_x(h, c, b, engine):
+            x_wide = work.tile([P, 2, SPAN], BF16, name="x_wide", bufs=6)
+            for i in range(2):
+                for q in range(SPAN // P):
+                    cols = slice(P * q, P * (q + 1))
+                    column = BLOCKS * i + (SPAN // P) * c + q
+                    values = tiles["x_bytes", h, b, c][:, i, cols].bitcast(FP8)
+                    scale = tiles["x_scale", 2 * h + b][:, column : column + 1]
+                    if engine == "vector":
+                        nc.vector.tensor_scalar(
+                            out=x_wide[:, i, cols], in0=values, scalar1=scale, scalar2=None, op0=ALU.mult
+                        )
+                    else:
+                        nc.scalar.activation(out=x_wide[:, i, cols], in_=values, func=ACT.Copy, scale=scale)
+            tiles["x_wide", h, c, b] = x_wide
+
+        def turn_x(h, c, b):
+            bank = take_bank(("x_turned", h, c, b), [P, 2, 2, P])
+            for i in range(2):
+                k_pairs = tiles["x_wide", h, c, b][:, i, :].bitcast(F32)
+                for u in range(2):
+                    nc.tensor.transpose(bank[:, i, u, :], k_pairs[:, u : SPAN // 2 : 2], identity[:])
+
+        def copy_x(h, c, b):
+            if b == 0:
+                tiles["x_grouped", h, c] = work.tile(
+                    [P, 2, PAIR * PACK], BF16, name="x_grouped", bufs=PASSES, align_bytes=64
+                )
+            out = tiles["x_grouped", h, c][:, b, :].bitcast(F32).rearrange("p (r i u) -> p r i u", i=2, u=2)
+            nc.scalar.copy(out=out, in_=tiles["x_turned", h, c, b][:].rearrange("p i u r -> p r i u"))
+            free_bank(("x_turned", h, c, b))
+
+        def quantize_x(h, c):
+            codes = keep.tile([P, SPAN], U32, name="x_codes_%d_%d" % (h, c), align_bytes=64)
+            scales = keep.tile([P, SPAN], U8, name="x_scale_bytes_%d_%d" % (h, c), align_bytes=64)
+            quantize(tiles["x_grouped", h, c][:].rearrange("p b f -> p (b f)"), codes[:], scales[:])
+            tiles["x_mx", h, c] = (codes, scales)
+
+
+        def interleave_w(g, w, c, engine, first=0, end=RUNS):
             if first == 0:
-                codes = keep.tile([P, SPAN], U32, name="x_codes_%d_%d" % (h, c), align_bytes=64)
-                scales = keep.tile([P, SPAN], U8, name="x_mxscales_%d_%d" % (h, c), align_bytes=64)
-                tiles["xq", h, c] = (codes, scales)
-            codes, scales = tiles["xq", h, c]
-            cols = slice(2 * P * first, 2 * P * (first + pairs))
-            source = tiles["xgrp", h, c][:, first : first + pairs, :].rearrange("p b f -> p (b f)")
-            quantize(source, codes[:, cols], scales[:, cols])
+                tiles["w_grouped", g, w, c] = work.tile(
+                    [P, SPAN * PACK], BF16, name="w_grouped", bufs=4, align_bytes=64
+                )
+            out = tiles["w_grouped", g, w, c][:].rearrange("p (t a e j) -> p a t e j", t=PACK, e=2, j=PACK)
+            in_ = tiles["w_rows", g, w, c][:].rearrange("p j (a e t) -> p a t e j", t=PACK, e=2)
+            copy_on(engine, out[:, first:end], in_[:, first:end])
 
-        def mix_w(g, w, c, engine, lo=0, hi=64):
-            if ("wgrp", g, w, c) not in tiles:
-                tiles["wgrp", g, w, c] = work.tile([P, SPAN * PACK], BF16, name="w_grouped", bufs=4, align_bytes=64)
-            out = tiles["wgrp", g, w, c][:].rearrange("p (t a b j) -> p a t b j", t=PACK, b=2, j=PACK)
-            in_ = tiles["wraw", g, w, c][:].rearrange("p j (a b t) -> p a t b j", t=PACK, b=2)
-            copy_on(engine, out[:, lo:hi], in_[:, lo:hi])
-
-        def quant_w(g, w, c):
+        def quantize_w(g, w, c):
             codes = keep.tile([P, SPAN], U32, name="w_codes_%d_%d_%d" % (g, w, c), align_bytes=64)
-            scales = keep.tile([P, SPAN], U8, name="w_mxscales_%d_%d_%d" % (g, w, c), align_bytes=64)
-            quantize(tiles["wgrp", g, w, c][:], codes[:], scales[:])
-            tiles["wq", g, w, c] = (codes, scales)
+            scales = keep.tile([P, SPAN], U8, name="w_scale_bytes_%d_%d_%d" % (g, w, c), align_bytes=64)
+            quantize(tiles["w_grouped", g, w, c][:], codes[:], scales[:])
+            tiles["w_mx", g, w, c] = (codes, scales)
 
-        def multiply(g, h, w, t, c, step, cols=slice(0, SPAN)):
-            key = ("acc", g, h, w, t, cols.start)
+
+        def multiply(g, h, w, t, c, step, cols):
+            key = ("sum", g, h, w, t, cols.start)
             if step == 0:
-                tiles[key] = psum.tile([P, SPAN], F32, name="bank_%d" % sum_banks.pop(0))
-            w_codes, w_scales = tiles["wq", g, w, c]
-            x_codes, x_scales = tiles["xq", h, c]
+                take_bank(key, [P, cols.stop - cols.start])
+            w_codes, w_scales = tiles["w_mx", g, w, c]
+            x_codes, x_scales = tiles["x_mx", h, c]
             units = slice(P * t, P * (t + 1))
             nc.tensor.matmul_mx(
-                out=tiles[key][:, : cols.stop - cols.start],
+                out=tiles[key][:],
                 lhsT=w_codes[:, units].bitcast(FP8X4),
                 lhsT_scale=w_scales[:, units],
                 rhs=x_codes[:, cols].bitcast(FP8X4),
@@ -140,92 +168,112 @@ def tile_maxout_patch_layer_b1_kernel(tc, X_bytes, X_scale, W1, W2, b1, b2, out_
 
         def one_pass(g, h, w, c, step):
             for t in range(PACK):
-                multiply(g, h, w, t, c, step)
+                multiply(g, h, w, t, c, step, ALL)
 
-        def product(g, h, w, t, cols=slice(0, SPAN)):
+        def whole_sum(g, h, w, t, cols=ALL):
             for c in range(PASSES):
                 multiply(g, h, w, t, c, c, cols)
 
-        def first_piece(g, h, t, cols=slice(0, SPAN)):
+        def first_piece(g, h, t, cols=ALL):
             if cols.start == 0:
-                tiles["piece", g, h, t] = work.tile([P, SPAN], F32, name="piece", bufs=8)
+                tiles["piece", g, h, t] = work.tile([P, SPAN], F32, name="piece", bufs=2 * PACK)
+            key = ("sum", g, h, 0, t, cols.start)
             nc.scalar.activation(
                 out=tiles["piece", g, h, t][:, cols],
-                in_=tiles["acc", g, h, 0, t, cols.start][:, : cols.stop - cols.start],
+                in_=tiles[key][:],
                 func=ACT.Identity,
                 bias=tiles["bias", 0][:, g, t : t + 1],
             )
+            free_bank(key)
 
-        def maxout(g, h, t, cols=slice(0, SPAN)):
-            width = cols.stop - cols.start
+        def maxout(g, h, t, cols=ALL):
             if t == 0:
-                y_units = work.tile([P, PACK, width], F32, name="y_units_%d_%d_%d" % (g, h, cols.start), bufs=1)
+                y_units = keep.tile(
+                    [P, PACK, cols.stop - cols.start], F32, name="y_units_%d_%d_%d" % (g, h, cols.start)
+                )
+                tiles["y_units", g, h, cols.start] = y_units
                 for i in range(cols.start // P, cols.stop // P):
-                    tiles["yt", g, h, i] = (y_units, P * i - cols.start)
+                    tiles["y_patches", g, h, i] = y_units[:, :, P * i - cols.start : P * (i + 1) - cols.start]
+            key = ("sum", g, h, 1, t, cols.start)
             nc.vector.scalar_tensor_tensor(
-                out=tiles["yt", g, h, cols.start // P][0][:, t, :],
-                in0=tiles["acc", g, h, 1, t, cols.start][:, : cols.stop - cols.start],
+                out=tiles["y_units", g, h, cols.start][:, t, :],
+                in0=tiles[key][:],
                 scalar=tiles["bias", 1][:, g, t : t + 1],
                 in1=tiles["piece", g, h, t][:, cols],
                 op0=ALU.add,
                 op1=ALU.max,
             )
+            free_bank(key)
 
-        def turn_y(g, h, i):
-            bank = psum.tile([P, PACK, P], F32, name="bank_%d" % y_banks.pop(0))
-            y_units, offset = tiles["yt", g, h, i]
+        def first_pieces(g, h, cols=ALL):
             for t in range(PACK):
-                nc.tensor.transpose(bank[:, t, :], y_units[:, t, offset : offset + P], ident[:])
-            tiles["ybank", g, h, i] = bank
+                whole_sum(g, h, 0, t, cols)
+                first_piece(g, h, t, cols)
 
-        def store_y(g, h, i, engine):
-            rows = work.tile([P, P, PACK], F32, name="y_rows", bufs=6)
-            copy_on(engine, rows[:], tiles["ybank", g, h, i][:].rearrange("p t m -> p m t"))
-            first = SPAN * h + P * i
-            nc.sync.dma_start(
-                out=out_0[first : first + P, SPAN * g : SPAN * (g + 1)], in_=rows[:].rearrange("p m t -> p (m t)")
+        def second_pieces(g, h, cols):
+            for t in range(PACK):
+                whole_sum(g, h, 1, t, cols)
+                maxout(g, h, t, cols)
+
+
+        def store_rows(g, h, i, queue=nc.sync):
+            key = ("y_turned", g, h, i)
+            bank = take_bank(key, [P, PACK, P])
+            for t in range(PACK):
+                nc.tensor.transpose(bank[:, t, :], tiles["y_patches", g, h, i][:, t, :], identity[:])
+            y_rows = work.tile([P, P, PACK], F32, name="y_rows", bufs=6)
+            nc.scalar.copy(out=y_rows[:], in_=bank[:].rearrange("p t m -> p m t"))
+            free_bank(key)
+            patch = SPAN * h + P * i
+            queue.dma_start(
+                out=out_0[patch : patch + P, SPAN * g : SPAN * (g + 1)], in_=y_rows[:].rearrange("p m t -> p (m t)")
             )
 
-        def round_y(g, h, engine, cols=slice(0, SPAN)):
-            grouped = work.tile([P, PACK * (cols.stop - cols.start)], BF16, name="y_grouped", bufs=3, align_bytes=64)
-            out = grouped[:].rearrange("p (c i t) -> p c i t", i=4, t=PACK)
-            in_ = tiles["yt", g, h, cols.start // P][0][:].rearrange("p t (c i) -> p c i t", i=4)
-            copy_on(engine, out, in_)
-            tiles["ygrp", g, h, cols.start] = grouped
+        def round_y(g, h, engine, cols=ALL):
+            y_grouped = work.tile(
+                [P, cols.stop - cols.start, PACK], BF16, name="y_grouped", bufs=3, align_bytes=64
+            )
+            copy_on(engine, y_grouped[:], tiles["y_units", g, h, cols.start][:].rearrange("p t m -> p m t"))
+            tiles["y_grouped", g, h, cols.start] = y_grouped
 
-        def quant_y(g, h, cols=slice(0, SPAN)):
-            if h == 0 and cols.start == 0:
-                tiles["yq", g] = keep.tile([P, T], U32, name="y_codes_%d" % g, align_bytes=64)
-                tiles["ys", g] = keep.tile([P, T], U8, name="y_mxscales_%d" % g, align_bytes=64)
-            tokens = slice(SPAN * h + cols.start, SPAN * h + cols.stop)
-            source = tiles["ygrp", g, h, cols.start][:]
-            quantize(source, tiles["yq", g][:, tokens], tiles["ys", g][:, tokens])
+        def quantize_y(g, h, cols=ALL):
+            if h == 0:
+                tiles["y_codes", g] = keep.tile([P, T], U32, name="y_codes_%d" % g, align_bytes=64)
+                tiles["y_scales", g] = keep.tile([P, T], U8, name="y_scale_bytes_%d" % g, align_bytes=64)
+            patches = slice(SPAN * h + cols.start, SPAN * h + cols.stop)
+            source = tiles["y_grouped", g, h, cols.start][:].rearrange("p m t -> p (m t)")
+            quantize(source, tiles["y_codes", g][:, patches], tiles["y_scales", g][:, patches])
+
+        def store_codes(g, h, cols=ALL):
+            patches = slice(SPAN * h + cols.start, SPAN * h + cols.stop)
             words = out_1[g].rearrange("p m t -> p (m t)").bitcast(I32)
-            nc.sync.dma_start(out=words[:, tokens], in_=tiles["yq", g][:, tokens].bitcast(I32))
+            nc.sync.dma_start(out=words[:, patches], in_=tiles["y_codes", g][:, patches].bitcast(I32))
 
         def store_scales(g):
-            for q in range(4):
+            for d in range(P // 32):
                 nc.sync.dma_start(
-                    out=out_2[g, 4 * q : 4 * q + 4, :].bitcast(I32),
-                    in_=tiles["ys", g][32 * q : 32 * q + 4, :].bitcast(I32),
+                    out=out_2[g, 4 * d : 4 * d + 4, :].bitcast(I32),
+                    in_=tiles["y_scales", g][32 * d : 32 * d + 4, :].bitcast(I32),
                 )
 
         def keep_warm(count):
+            bank = take_bank("warm", [P, SPAN])
             for step in range(count):
-                nc.tensor.matmul(out=idle_bank[:], lhsT=zeros[:, :P], rhs=zeros[:], start=True, stop=True)
+                nc.tensor.matmul(out=bank[:], lhsT=zeros[:, :P], rhs=zeros[:], start=True, stop=True)
+            free_bank("warm")
 
         zeros = keep.tile([P, SPAN], BF16, name="zeros")
         nc.vector.memset(zeros[:], 0.0)
-        idle_bank = psum.tile([P, SPAN], F32, name="bank_4")
-        ident = keep.tile([P, P], F32, name="ident")
-        make_identity(nc, ident[:])
+        identity = keep.tile([P, P], F32, name="identity")
+        make_identity(nc, identity[:])
 
-        load_scales()
-        load_x(0, 0)
-        load_w(0, 0, 0)
+        load_x_scales(0, 1)
+        load_x(0, 0, 0, 1)
+        load_x(0, 0, 1, PASSES - 1)
+        load_x_scales(1, T // PAIR - 1)
         load_x(0, 1)
-        load_w(0, 0, 1)
-        load_w(0, 0, 2)
+        for c in range(PASSES):
+            load_w(0, 0, c)
         load_x(1, 0)
         load_x(1, 1)
         load_bias(0)
@@ -236,141 +284,134 @@ def tile_maxout_patch_layer_b1_kernel(tc, X_bytes, X_scale, W1, W2, b1, b2, out_
             for c in range(PASSES):
                 load_w(1, w, c)
 
-        low, high = slice(0, 2 * P), slice(2 * P, SPAN)
-        third, last = slice(2 * P, 3 * P), slice(3 * P, SPAN)
-
-        def finish_rows(g, h, engines="SSSS", which=range(4)):
-            for i in which:
-                turn_y(g, h, i)
-                store_y(g, h, i, engines[i])
-
-        widen(0, 0, 0, "V")
-        widen(0, 1, 0, "S")
-        widen(0, 2, 0, "V")
-        keep_warm(6)
+        keep_warm(WARM_FIRST)
+        for c, engine in enumerate(("vector", "scalar", "vector")):
+            widen_x(0, c, 0, engine)
         for c in range(PASSES):
             turn_x(0, c, 0)
-            copy_x(0, c, 0, "S")
-        keep_warm(3)
-        mix_w(0, 0, 0, "V")
-        mix_w(0, 0, 1, "S", 0, 32)
-        for c in range(PASSES):
-            widen(0, c, 1, "V")
-            if c == 2:
-                keep_warm(2)
+            copy_x(0, c, 0)
+        keep_warm(WARM_BETWEEN)
+        for c in range(2):
+            widen_x(0, c, 1, "vector")
             turn_x(0, c, 1)
-            copy_x(0, c, 1, "S")
-            if c == 1:
-                quant_w(0, 0, 0)
-        quant_x(0, 0)
+        interleave_w(0, 0, 0, "vector")
+        interleave_w(0, 0, 1, "scalar", 0, RUNS // 2)
+        copy_x(0, 0, 1)
+        copy_x(0, 1, 1)
+        interleave_w(0, 0, 1, "scalar", RUNS // 2, RUNS)
+        keep_warm(WARM_BETWEEN)
+        widen_x(0, 2, 1, "vector")
+        turn_x(0, 2, 1)
+        copy_x(0, 2, 1)
+        quantize_w(0, 0, 0)
+        quantize_x(0, 0)
         one_pass(0, 0, 0, 0, 0)
-        mix_w(0, 0, 1, "S", 32, 64)
-        quant_x(0, 1)
-        mix_w(0, 0, 2, "V", 0, 32)
-        mix_w(0, 0, 2, "S", 32, 64)
-        quant_x(0, 2)
-        quant_w(0, 0, 1)
-        one_pass(0, 0, 0, 1, 1)
+        interleave_w(0, 0, 2, "vector", 0, CUT_FIRST_W1)
+        interleave_w(0, 0, 2, "scalar", CUT_FIRST_W1, RUNS)
+        for c in (1, 2):
+            quantize_x(0, c)
+            quantize_w(0, 0, c)
+            one_pass(0, 0, 0, c, c)
+
+        interleave_w(0, 1, 0, "scalar")
         for b in range(2):
-            widen(1, 0, b, "V")
+            widen_x(1, 0, b, "vector")
             turn_x(1, 0, b)
-        quant_w(0, 0, 2)
-        one_pass(0, 0, 0, 2, 2)
-        mix_w(0, 1, 0, "S")
+        first_piece(0, 0, 0)
+        copy_x(1, 0, 0)
+        copy_x(1, 0, 1)
+        keep_warm(WARM_BETWEEN)
         for b in range(2):
-            copy_x(1, 0, b, "S")
-            widen(1, 1, b, "V")
+            widen_x(1, 1, b, "vector")
             turn_x(1, 1, b)
-        widen(1, 2, 0, "V")
-        widen(1, 2, 1, "V")
-        turn_x(1, 2, 0)
-        quant_x(1, 0)
-        for t in range(PACK):
-            first_piece(0, 0, t)
-        copy_x(1, 1, 0, "V")
-        copy_x(1, 1, 1, "V")
+        widen_x(1, 2, 0, "vector")
+        quantize_x(1, 0)
+        widen_x(1, 2, 1, "vector")
+        first_piece(0, 0, 1)
+        first_piece(0, 0, 2)
+        copy_x(1, 1, 0)
+        copy_x(1, 1, 1)
+        first_piece(0, 0, 3)
         one_pass(0, 1, 0, 0, 0)
-        turn_x(1, 2, 1)
-        copy_x(1, 2, 0, "S")
-        mix_w(0, 1, 1, "S", 0, 32)
-        copy_x(1, 2, 1, "S")
-        quant_w(0, 1, 0)
-        quant_x(1, 1)
+        for b in range(2):
+            turn_x(1, 2, b)
+            copy_x(1, 2, b)
+        quantize_w(0, 1, 0)
+        quantize_x(1, 1)
         one_pass(0, 1, 0, 1, 1)
-        mix_w(0, 1, 1, "S", 32, 64)
+
+        interleave_w(0, 1, 1, "vector", 0, CUT_FIRST_W2)
+        interleave_w(0, 1, 1, "scalar", CUT_FIRST_W2, RUNS)
         one_pass(0, 0, 1, 0, 0)
-        mix_w(0, 1, 2, "V")
-        quant_x(1, 2)
+        interleave_w(0, 1, 2, "vector")
+        quantize_x(1, 2)
         one_pass(0, 1, 0, 2, 2)
         for t in range(PACK):
             first_piece(0, 1, t)
         for step, c in ((1, 2), (2, 1)):
-            quant_w(0, 1, c)
+            quantize_w(0, 1, c)
             one_pass(0, 0, 1, c, step)
-        mix_w(1, 0, 0, "V")
-        mix_w(1, 0, 2, "V", 0, 32)
-        mix_w(1, 0, 1, "S")
+
+        interleave_w(1, 0, 0, "vector")
+        interleave_w(1, 0, 2, "vector", 0, CUT_SECOND_W1)
+        interleave_w(1, 0, 1, "scalar")
         for t in range(PACK):
             maxout(0, 0, t)
-        quant_w(1, 0, 0)
-        mix_w(1, 0, 2, "S", 32, 64)
-        quant_w(1, 0, 1)
+        quantize_w(1, 0, 0)
+        interleave_w(1, 0, 2, "scalar", CUT_SECOND_W1, RUNS)
+        quantize_w(1, 0, 1)
         for t in range(PACK):
-            product(0, 1, 1, t)
+            whole_sum(0, 1, 1, t)
             maxout(0, 1, t)
             if t == 1:
-                quant_w(1, 0, 2)
-        mix_w(1, 1, 0, "S")
-        finish_rows(0, 0, "SSSS", (0, 1))
-        mix_w(1, 1, 1, "V")
-        quant_w(1, 1, 0)
-        mix_w(1, 1, 2, "V")
-        for t in range(PACK):
-            product(1, 0, 0, t)
-            first_piece(1, 0, t)
-        finish_rows(0, 0, "SSSS", (2, 3))
-        for c in range(PASSES):
-            if c > 0:
-                quant_w(1, 1, c)
+                quantize_w(1, 0, 2)
+
+        interleave_w(1, 1, 0, "scalar")
+        store_rows(0, 0, 0)
+        store_rows(0, 0, 1)
+        interleave_w(1, 1, 1, "vector")
+        quantize_w(1, 1, 0)
+        interleave_w(1, 1, 2, "vector")
+        first_pieces(1, 0)
+        one_pass(1, 0, 1, 0, 0)
+        for h, i in ((0, 2), (0, 3), (1, 0), (1, 1)):
+            store_rows(0, h, i)
+        for c in (1, 2):
+            quantize_w(1, 1, c)
             one_pass(1, 0, 1, c, c)
-        round_y(0, 0, "V")
-        finish_rows(0, 1, "SSSS", (0, 1))
+        round_y(0, 0, "vector")
         for t in range(PACK):
             maxout(1, 0, t)
             if t == 0:
-                quant_y(0, 0)
-        round_y(0, 1, "V")
-        for t in range(PACK):
-            product(1, 1, 0, t)
-            first_piece(1, 1, t)
-        round_y(1, 0, "V")
-        quant_y(0, 1)
-        turn_y(0, 1, 2)
-        turn_y(0, 1, 3)
-        turn_y(1, 0, 0)
-        turn_y(1, 0, 1)
-        store_y(0, 1, 2, "S")
-        store_y(0, 1, 3, "S")
-        store_y(1, 0, 0, "S")
-        store_y(1, 0, 1, "S")
+                quantize_y(0, 0)
+                store_codes(0, 0)
+        round_y(0, 1, "vector")
+
+        first_pieces(1, 1, LOW)
+        for g, h, i in ((0, 1, 2), (0, 1, 3), (1, 0, 0), (1, 0, 1)):
+            store_rows(g, h, i)
+        quantize_y(0, 1)
+        store_codes(0, 1)
         store_scales(0)
-        quant_y(1, 0)
-        for t in range(PACK):
-            product(1, 1, 1, t, low)
-            maxout(1, 1, t, low)
-        finish_rows(1, 0, "SSSS", (2, 3))
-        round_y(1, 1, "V", low)
-        for t in range(PACK):
-            product(1, 1, 1, t, high)
-            if t == 0:
-                quant_y(1, 1, low)
-            if t == 1:
-                finish_rows(1, 1, "SSSS", (0, 1))
-            maxout(1, 1, t, high)
-        round_y(1, 1, "V", high)
-        turn_y(1, 1, 2)
-        turn_y(1, 1, 3)
-        store_y(1, 1, 2, "S")
-        quant_y(1, 1, high)
-        store_y(1, 1, 3, "S")
+        second_pieces(1, 1, LOW)
+        store_rows(1, 0, 2)
+        store_rows(1, 0, 3)
+        round_y(1, 0, "vector")
+        first_pieces(1, 1, HIGH)
+        round_y(1, 1, "vector", LOW)
+        quantize_y(1, 0)
+        store_codes(1, 0)
+        store_rows(1, 1, 0)
+        store_rows(1, 1, 1)
+        quantize_y(1, 1, LOW)
+        store_codes(1, 1, LOW)
+        second_pieces(1, 1, THIRD)
+        round_y(1, 1, "scalar", THIRD)
+        second_pieces(1, 1, LAST)
+        store_rows(1, 1, 2)
+        round_y(1, 1, "vector", LAST)
+        quantize_y(1, 1, THIRD)
+        store_rows(1, 1, 3, nc.scalar)
+        quantize_y(1, 1, LAST)
+        store_codes(1, 1, HIGH)
         store_scales(1)

@@ -31,7 +31,6 @@ WARM_FIRST, WARM_BETWEEN = 6, 2
 
 ALL = slice(0, SPAN)
 LOW, HIGH = slice(0, PAIR), slice(PAIR, SPAN)
-THIRD, LAST = slice(PAIR, 3 * P), slice(3 * P, SPAN)
 
 
 def tile_maxout_patch_layer_b1_kernel(tc, X_bytes, X_scale, W1, W2, b1, b2, out_0, out_1, out_2):
@@ -67,20 +66,16 @@ def tile_maxout_patch_layer_b1_kernel(tc, X_bytes, X_scale, W1, W2, b1, b2, out_
             nc.vector.quantize_mx(out=codes.bitcast(FP8X4), scales=scales, in_=source)
 
 
-        def load_x_scales(first, count):
-            x_scale = keep.tile([P, count, 2 * BLOCKS], F32, name="x_scale_%d" % first)
-            rows = X_scale[PAIR * first : PAIR * (first + count), :]
-            nc.scalar.dma_start(out=x_scale[:], in_=rows.rearrange("(d p i) j -> p d (i j)", p=P, i=2))
-            for d in range(count):
-                tiles["x_scale", first + d] = x_scale[:, d, :]
+        def load_x_scales():
+            x_scale = keep.tile([P, T // PAIR, 2 * BLOCKS], F32, name="x_scale")
+            nc.scalar.dma_start(out=x_scale[:], in_=X_scale.rearrange("(d p i) j -> p d (i j)", p=P, i=2))
+            tiles["x_scale"] = x_scale
 
-        def load_x(h, b, first=0, count=PASSES):
-            x_bytes = keep.tile([P, 2, SPAN * count], U8, name="x_bytes_%d_%d_%d" % (h, b, first))
+        def load_x(h, b):
+            x_bytes = keep.tile([P, 2 * K], U8, name="x_bytes_%d_%d" % (h, b))
             patch = SPAN * h + PAIR * b
-            rows = X_bytes[patch : patch + PAIR, SPAN * first : SPAN * (first + count)]
-            nc.sync.dma_start(out=x_bytes[:], in_=rows.rearrange("(p i) k -> p i k", i=2))
-            for c in range(count):
-                tiles["x_bytes", h, b, first + c] = x_bytes[:, :, SPAN * c : SPAN * (c + 1)]
+            nc.sync.dma_start(out=x_bytes[:], in_=X_bytes[patch : patch + PAIR, :].rearrange("(p i) k -> p (i k)", i=2))
+            tiles["x_bytes", h, b] = x_bytes
 
         def load_w(g, w, c):
             w_rows = keep.tile([P, PACK, SPAN], BF16, name="w_rows_%d_%d_%d" % (g, w, c))
@@ -99,9 +94,9 @@ def tile_maxout_patch_layer_b1_kernel(tc, X_bytes, X_scale, W1, W2, b1, b2, out_
             for i in range(2):
                 for q in range(SPAN // P):
                     cols = slice(P * q, P * (q + 1))
-                    column = BLOCKS * i + (SPAN // P) * c + q
-                    values = tiles["x_bytes", h, b, c][:, i, cols].bitcast(FP8)
-                    scale = tiles["x_scale", 2 * h + b][:, column : column + 1]
+                    block = BLOCKS * i + (SPAN // P) * c + q
+                    values = tiles["x_bytes", h, b][:, P * block : P * (block + 1)].bitcast(FP8)
+                    scale = tiles["x_scale"][:, 2 * h + b, block : block + 1]
                     if engine == "vector":
                         nc.vector.tensor_scalar(
                             out=x_wide[:, i, cols], in0=values, scalar1=scale, scalar2=None, op0=ALU.mult
@@ -166,8 +161,8 @@ def tile_maxout_patch_layer_b1_kernel(tc, X_bytes, X_scale, W1, W2, b1, b2, out_
                 stop=(step == PASSES - 1),
             )
 
-        def one_pass(g, h, w, c, step):
-            for t in range(PACK):
+        def one_pass(g, h, w, c, step, places=range(PACK)):
+            for t in places:
                 multiply(g, h, w, t, c, step, ALL)
 
         def whole_sum(g, h, w, t, cols=ALL):
@@ -267,13 +262,12 @@ def tile_maxout_patch_layer_b1_kernel(tc, X_bytes, X_scale, W1, W2, b1, b2, out_
         identity = keep.tile([P, P], F32, name="identity")
         make_identity(nc, identity[:])
 
-        load_x_scales(0, 1)
-        load_x(0, 0, 0, 1)
-        load_x(0, 0, 1, PASSES - 1)
-        load_x_scales(1, T // PAIR - 1)
+        load_x_scales()
+        load_x(0, 0)
+        load_w(0, 0, 0)
         load_x(0, 1)
-        for c in range(PASSES):
-            load_w(0, 0, c)
+        load_w(0, 0, 1)
+        load_w(0, 0, 2)
         load_x(1, 0)
         load_x(1, 1)
         load_bias(0)
@@ -291,28 +285,29 @@ def tile_maxout_patch_layer_b1_kernel(tc, X_bytes, X_scale, W1, W2, b1, b2, out_
             turn_x(0, c, 0)
             copy_x(0, c, 0)
         keep_warm(WARM_BETWEEN)
+        interleave_w(0, 0, 0, "vector")
+        interleave_w(0, 0, 1, "scalar", 0, RUNS // 2)
         for c in range(2):
             widen_x(0, c, 1, "vector")
             turn_x(0, c, 1)
-        interleave_w(0, 0, 0, "vector")
-        interleave_w(0, 0, 1, "scalar", 0, RUNS // 2)
-        copy_x(0, 0, 1)
-        copy_x(0, 1, 1)
+            copy_x(0, c, 1)
+        quantize_w(0, 0, 0)
         interleave_w(0, 0, 1, "scalar", RUNS // 2, RUNS)
         keep_warm(WARM_BETWEEN)
         widen_x(0, 2, 1, "vector")
         turn_x(0, 2, 1)
         copy_x(0, 2, 1)
-        quantize_w(0, 0, 0)
         quantize_x(0, 0)
         one_pass(0, 0, 0, 0, 0)
         interleave_w(0, 0, 2, "vector", 0, CUT_FIRST_W1)
         interleave_w(0, 0, 2, "scalar", CUT_FIRST_W1, RUNS)
-        for c in (1, 2):
-            quantize_x(0, c)
-            quantize_w(0, 0, c)
-            one_pass(0, 0, 0, c, c)
+        quantize_x(0, 1)
+        quantize_w(0, 0, 1)
+        one_pass(0, 0, 0, 1, 1)
+        quantize_x(0, 2)
+        quantize_w(0, 0, 2)
 
+        one_pass(0, 0, 0, 2, 2, (0, 1))
         interleave_w(0, 1, 0, "scalar")
         for b in range(2):
             widen_x(1, 0, b, "vector")
@@ -320,7 +315,7 @@ def tile_maxout_patch_layer_b1_kernel(tc, X_bytes, X_scale, W1, W2, b1, b2, out_
         first_piece(0, 0, 0)
         copy_x(1, 0, 0)
         copy_x(1, 0, 1)
-        keep_warm(WARM_BETWEEN)
+        one_pass(0, 0, 0, 2, 2, (2, 3))
         for b in range(2):
             widen_x(1, 1, b, "vector")
             turn_x(1, 1, b)
@@ -405,13 +400,10 @@ def tile_maxout_patch_layer_b1_kernel(tc, X_bytes, X_scale, W1, W2, b1, b2, out_
         store_rows(1, 1, 1)
         quantize_y(1, 1, LOW)
         store_codes(1, 1, LOW)
-        second_pieces(1, 1, THIRD)
-        round_y(1, 1, "scalar", THIRD)
-        second_pieces(1, 1, LAST)
+        second_pieces(1, 1, HIGH)
+        round_y(1, 1, "vector", HIGH)
         store_rows(1, 1, 2)
-        round_y(1, 1, "vector", LAST)
-        quantize_y(1, 1, THIRD)
         store_rows(1, 1, 3, nc.scalar)
-        quantize_y(1, 1, LAST)
+        quantize_y(1, 1, HIGH)
         store_codes(1, 1, HIGH)
         store_scales(1)

from contextlib import ExitStack

import concourse.mybir as mybir
from concourse.masks import make_identity

T, K, N = 1024, 1536, 1024
FLOPS = 2 * T * K * 2 * N

F32 = mybir.dt.float32
BF16 = mybir.dt.bfloat16
U32 = mybir.dt.uint32
I32 = mybir.dt.int32
U8 = mybir.dt.uint8
FP8 = mybir.dt.float8_e4m3fn
FP8X4 = mybir.dt.float8_e4m3fn_x4
ALU = mybir.AluOpType
ACT = mybir.ActivationFunctionType

P = 128
PACK = 4
SPAN = P * PACK
PAIR = 2 * P
PASSES = K // SPAN
BLOCKS = K // P
BANKS = 8
RUNS = SPAN // 8

CUT_FIRST_W1, CUT_FIRST_W2, CUT_SECOND_W1 = 48, 16, 32

WARM_FIRST, WARM_BETWEEN = 6, 2

ALL = slice(0, SPAN)
LOW, HIGH = slice(0, PAIR), slice(PAIR, SPAN)


def tile_maxout_patch_layer_b1_kernel(tc, X_bytes, X_scale, W1, W2, b1, b2, out_0, out_1, out_2):
    nc = tc.nc
    weights = (W1, W2)
    biases = (b1, b2)

    with ExitStack() as ctx:
        keep = ctx.enter_context(tc.tile_pool(name="keep", bufs=1))
        work = ctx.enter_context(tc.tile_pool(name="work", bufs=1))
        psum = ctx.enter_context(tc.psum_pool(name="psum", bufs=1))
        ctx.enter_context(tc.manual_schedule())

        tiles = {}
        free_banks = list(range(BANKS))

        def take_bank(key, shape):
            number = free_banks.pop(0)
            tiles[key] = psum.tile(shape, F32, name="bank_%d" % number)
            tiles["bank of", key] = number
            return tiles[key]

        def free_bank(key):
            free_banks.append(tiles["bank of", key])

        def copy_on(engine, out, in_):
            if engine == "vector":
                nc.vector.tensor_copy(out=out, in_=in_)
            else:
                nc.scalar.copy(out=out, in_=in_)

        def quantize(source, codes, scales):
            nc.vector.quantize_mx(out=codes.bitcast(FP8X4), scales=scales, in_=source)


        def load_x_scales():
            x_scale = keep.tile([P, T // PAIR, 2 * BLOCKS], F32, name="x_scale")
            nc.scalar.dma_start(out=x_scale[:], in_=X_scale.rearrange("(d p i) j -> p d (i j)", p=P, i=2))
            tiles["x_scale"] = x_scale

        def load_x(h, b):
            x_bytes = keep.tile([P, 2 * K], U8, name="x_bytes_%d_%d" % (h, b))
            patch = SPAN * h + PAIR * b
            nc.sync.dma_start(out=x_bytes[:], in_=X_bytes[patch : patch + PAIR, :].rearrange("(p i) k -> p (i k)", i=2))
            tiles["x_bytes", h, b] = x_bytes

        def load_w(g, w, c):
            w_rows = keep.tile([P, PACK, SPAN], BF16, name="w_rows_%d_%d_%d" % (g, w, c))
            rows = weights[w][SPAN * c : SPAN * (c + 1), SPAN * g : SPAN * (g + 1)]
            nc.sync.dma_start(out=w_rows[:], in_=rows.rearrange("(p j) n -> p j n", j=PACK))
            tiles["w_rows", g, w, c] = w_rows

        def load_bias(w):
            bias = keep.tile([P, N // SPAN, 16], BF16, name="bias_%d" % w)
            nc.sync.dma_start(out=bias[:, :, :PACK], in_=biases[w].rearrange("(g p t) -> p g t", p=P, t=PACK))
            tiles["bias", w] = bias


        def widen_x(h, c, b, engine):
            x_wide = work.tile([P, 2, SPAN], BF16, name="x_wide", bufs=6)
            for i in range(2):
                for q in range(SPAN // P):
                    cols = slice(P * q, P * (q + 1))
                    block = BLOCKS * i + (SPAN // P) * c + q
                    values = tiles["x_bytes", h, b][:, P * block : P * (block + 1)].bitcast(FP8)
                    scale = tiles["x_scale"][:, 2 * h + b, block : block + 1]
                    if engine == "vector":
                        nc.vector.tensor_scalar(
                            out=x_wide[:, i, cols], in0=values, scalar1=scale, scalar2=None, op0=ALU.mult
                        )
                    else:
                        nc.scalar.activation(out=x_wide[:, i, cols], in_=values, func=ACT.Copy, scale=scale)
            tiles["x_wide", h, c, b] = x_wide

        def turn_x(h, c, b):
            bank = take_bank(("x_turned", h, c, b), [P, 2, 2, P])
            for i in range(2):
                k_pairs = tiles["x_wide", h, c, b][:, i, :].bitcast(F32)
                for u in range(2):
                    nc.tensor.transpose(bank[:, i, u, :], k_pairs[:, u : SPAN // 2 : 2], identity[:])

        def copy_x(h, c, b):
            if b == 0:
                tiles["x_grouped", h, c] = work.tile(
                    [P, 2, PAIR * PACK], BF16, name="x_grouped", bufs=PASSES, align_bytes=64
                )
            out = tiles["x_grouped", h, c][:, b, :].bitcast(F32).rearrange("p (r i u) -> p r i u", i=2, u=2)
            nc.scalar.copy(out=out, in_=tiles["x_turned", h, c, b][:].rearrange("p i u r -> p r i u"))
            free_bank(("x_turned", h, c, b))

        def quantize_x(h, c):
            codes = keep.tile([P, SPAN], U32, name="x_codes_%d_%d" % (h, c), align_bytes=64)
            scales = keep.tile([P, SPAN], U8, name="x_scale_bytes_%d_%d" % (h, c), align_bytes=64)
            quantize(tiles["x_grouped", h, c][:].rearrange("p b f -> p (b f)"), codes[:], scales[:])
            tiles["x_mx", h, c] = (codes, scales)


        def interleave_w(g, w, c, engine, first=0, end=RUNS):
            if first == 0:
                tiles["w_grouped", g, w, c] = work.tile(
                    [P, SPAN * PACK], BF16, name="w_grouped", bufs=4, align_bytes=64
                )
            out = tiles["w_grouped", g, w, c][:].rearrange("p (t a e j) -> p a t e j", t=PACK, e=2, j=PACK)
            in_ = tiles["w_rows", g, w, c][:].rearrange("p j (a e t) -> p a t e j", t=PACK, e=2)
            copy_on(engine, out[:, first:end], in_[:, first:end])

        def quantize_w(g, w, c):
            codes = keep.tile([P, SPAN], U32, name="w_codes_%d_%d_%d" % (g, w, c), align_bytes=64)
            scales = keep.tile([P, SPAN], U8, name="w_scale_bytes_%d_%d_%d" % (g, w, c), align_bytes=64)
            quantize(tiles["w_grouped", g, w, c][:], codes[:], scales[:])
            tiles["w_mx", g, w, c] = (codes, scales)


        def multiply(g, h, w, t, c, step, cols):
            key = ("sum", g, h, w, t, cols.start)
            if step == 0:
                take_bank(key, [P, cols.stop - cols.start])
            w_codes, w_scales = tiles["w_mx", g, w, c]
            x_codes, x_scales = tiles["x_mx", h, c]
            units = slice(P * t, P * (t + 1))
            nc.tensor.matmul_mx(
                out=tiles[key][:],
                lhsT=w_codes[:, units].bitcast(FP8X4),
                lhsT_scale=w_scales[:, units],
                rhs=x_codes[:, cols].bitcast(FP8X4),
                rhs_scale=x_scales[:, cols],
                start=(step == 0),
                stop=(step == PASSES - 1),
            )

        def one_pass(g, h, w, c, step, places=range(PACK)):
            for t in places:
                multiply(g, h, w, t, c, step, ALL)

        def whole_sum(g, h, w, t, cols=ALL):
            for c in range(PASSES):
                multiply(g, h, w, t, c, c, cols)

        def first_piece(g, h, t, cols=ALL):
            if cols.start == 0:
                tiles["piece", g, h, t] = work.tile([P, SPAN], F32, name="piece", bufs=2 * PACK)
            key = ("sum", g, h, 0, t, cols.start)
            nc.scalar.activation(
                out=tiles["piece", g, h, t][:, cols],
                in_=tiles[key][:],
                func=ACT.Identity,
                bias=tiles["bias", 0][:, g, t : t + 1],
            )
            free_bank(key)

        def maxout(g, h, t, cols=ALL):
            if t == 0:
                y_units = keep.tile(
                    [P, PACK, cols.stop - cols.start], F32, name="y_units_%d_%d_%d" % (g, h, cols.start)
                )
                tiles["y_units", g, h, cols.start] = y_units
                for i in range(cols.start // P, cols.stop // P):
                    tiles["y_patches", g, h, i] = y_units[:, :, P * i - cols.start : P * (i + 1) - cols.start]
            key = ("sum", g, h, 1, t, cols.start)
            nc.vector.scalar_tensor_tensor(
                out=tiles["y_units", g, h, cols.start][:, t, :],
                in0=tiles[key][:],
                scalar=tiles["bias", 1][:, g, t : t + 1],
                in1=tiles["piece", g, h, t][:, cols],
                op0=ALU.add,
                op1=ALU.max,
            )
            free_bank(key)

        def first_pieces(g, h, cols=ALL):
            for t in range(PACK):
                whole_sum(g, h, 0, t, cols)
                first_piece(g, h, t, cols)

        def second_pieces(g, h, cols):
            for t in range(PACK):
                whole_sum(g, h, 1, t, cols)
                maxout(g, h, t, cols)


        def store_rows(g, h, i, queue=nc.sync):
            key = ("y_turned", g, h, i)
            bank = take_bank(key, [P, PACK, P])
            for t in range(PACK):
                nc.tensor.transpose(bank[:, t, :], tiles["y_patches", g, h, i][:, t, :], identity[:])
            y_rows = work.tile([P, P, PACK], F32, name="y_rows", bufs=6)
            nc.scalar.copy(out=y_rows[:], in_=bank[:].rearrange("p t m -> p m t"))
            free_bank(key)
            patch = SPAN * h + P * i
            queue.dma_start(
                out=out_0[patch : patch + P, SPAN * g : SPAN * (g + 1)], in_=y_rows[:].rearrange("p m t -> p (m t)")
            )

        def round_y(g, h, engine, cols=ALL):
            y_grouped = work.tile(
                [P, cols.stop - cols.start, PACK], BF16, name="y_grouped", bufs=3, align_bytes=64
            )
            copy_on(engine, y_grouped[:], tiles["y_units", g, h, cols.start][:].rearrange("p t m -> p m t"))
            tiles["y_grouped", g, h, cols.start] = y_grouped

        def quantize_y(g, h, cols=ALL):
            if h == 0:
                tiles["y_codes", g] = keep.tile([P, T], U32, name="y_codes_%d" % g, align_bytes=64)
                tiles["y_scales", g] = keep.tile([P, T], U8, name="y_scale_bytes_%d" % g, align_bytes=64)
            patches = slice(SPAN * h + cols.start, SPAN * h + cols.stop)
            source = tiles["y_grouped", g, h, cols.start][:].rearrange("p m t -> p (m t)")
            quantize(source, tiles["y_codes", g][:, patches], tiles["y_scales", g][:, patches])

        def store_codes(g, h, cols=ALL):
            patches = slice(SPAN * h + cols.start, SPAN * h + cols.stop)
            words = out_1[g].rearrange("p m t -> p (m t)").bitcast(I32)
            nc.sync.dma_start(out=words[:, patches], in_=tiles["y_codes", g][:, patches].bitcast(I32))

        def store_scales(g):
            for d in range(P // 32):
                nc.sync.dma_start(
                    out=out_2[g, 4 * d : 4 * d + 4, :].bitcast(I32),
                    in_=tiles["y_scales", g][32 * d : 32 * d + 4, :].bitcast(I32),
                )

        def keep_warm(count):
            bank = take_bank("warm", [P, SPAN])
            for step in range(count):
                nc.tensor.matmul(out=bank[:], lhsT=zeros[:, :P], rhs=zeros[:], start=True, stop=True)
            free_bank("warm")

        zeros = keep.tile([P, SPAN], BF16, name="zeros")
        nc.vector.memset(zeros[:], 0.0)
        identity = keep.tile([P, P], F32, name="identity")
        make_identity(nc, identity[:])

        load_x_scales()
        load_x(0, 0)
        load_w(0, 0, 0)
        load_x(0, 1)
        load_w(0, 0, 1)
        load_w(0, 0, 2)
        load_x(1, 0)
        load_x(1, 1)
        load_bias(0)
        for c in range(PASSES):
            load_w(0, 1, c)
        load_bias(1)
        for w in range(2):
            for c in range(PASSES):
                load_w(1, w, c)

        keep_warm(WARM_FIRST)
        for c, engine in enumerate(("vector", "scalar", "vector")):
            widen_x(0, c, 0, engine)
        for c in range(PASSES):
            turn_x(0, c, 0)
            copy_x(0, c, 0)
        keep_warm(WARM_BETWEEN)
        interleave_w(0, 0, 0, "vector")
        interleave_w(0, 0, 1, "scalar", 0, RUNS // 2)
        for c in range(2):
            widen_x(0, c, 1, "vector")
            turn_x(0, c, 1)
            copy_x(0, c, 1)
        quantize_w(0, 0, 0)
        interleave_w(0, 0, 1, "scalar", RUNS // 2, RUNS)
        keep_warm(WARM_BETWEEN)
        widen_x(0, 2, 1, "vector")
        turn_x(0, 2, 1)
        copy_x(0, 2, 1)
        quantize_x(0, 0)
        one_pass(0, 0, 0, 0, 0)
        interleave_w(0, 0, 2, "vector", 0, CUT_FIRST_W1)
        interleave_w(0, 0, 2, "scalar", CUT_FIRST_W1, RUNS)
        quantize_x(0, 1)
        quantize_w(0, 0, 1)
        one_pass(0, 0, 0, 1, 1)
        quantize_x(0, 2)
        quantize_w(0, 0, 2)

        one_pass(0, 0, 0, 2, 2, (0, 1))
        interleave_w(0, 1, 0, "scalar")
        for b in range(2):
            widen_x(1, 0, b, "vector")
            turn_x(1, 0, b)
        first_piece(0, 0, 0)
        copy_x(1, 0, 0)
        copy_x(1, 0, 1)
        one_pass(0, 0, 0, 2, 2, (2, 3))
        for b in range(2):
            widen_x(1, 1, b, "vector")
            turn_x(1, 1, b)
        widen_x(1, 2, 0, "vector")
        quantize_x(1, 0)
        widen_x(1, 2, 1, "vector")
        first_piece(0, 0, 1)
        first_piece(0, 0, 2)
        copy_x(1, 1, 0)
        copy_x(1, 1, 1)
        first_piece(0, 0, 3)
        one_pass(0, 1, 0, 0, 0)
        for b in range(2):
            turn_x(1, 2, b)
            copy_x(1, 2, b)
        quantize_w(0, 1, 0)
        quantize_x(1, 1)
        one_pass(0, 1, 0, 1, 1)

        interleave_w(0, 1, 1, "vector", 0, CUT_FIRST_W2)
        interleave_w(0, 1, 1, "scalar", CUT_FIRST_W2, RUNS)
        one_pass(0, 0, 1, 0, 0)
        interleave_w(0, 1, 2, "vector")
        quantize_x(1, 2)
        one_pass(0, 1, 0, 2, 2)
        for t in range(PACK):
            first_piece(0, 1, t)
        for step, c in ((1, 2), (2, 1)):
            quantize_w(0, 1, c)
            one_pass(0, 0, 1, c, step)

        interleave_w(1, 0, 0, "vector")
        interleave_w(1, 0, 2, "vector", 0, CUT_SECOND_W1)
        interleave_w(1, 0, 1, "scalar")
        for t in range(PACK):
            maxout(0, 0, t)
        quantize_w(1, 0, 0)
        interleave_w(1, 0, 2, "scalar", CUT_SECOND_W1, RUNS)
        quantize_w(1, 0, 1)
        for t in range(PACK):
            whole_sum(0, 1, 1, t)
            maxout(0, 1, t)
            if t == 1:
                quantize_w(1, 0, 2)

        interleave_w(1, 1, 0, "scalar")
        store_rows(0, 0, 0)
        store_rows(0, 0, 1)
        interleave_w(1, 1, 1, "vector")
        quantize_w(1, 1, 0)
        interleave_w(1, 1, 2, "vector")
        first_pieces(1, 0)
        one_pass(1, 0, 1, 0, 0)
        for h, i in ((0, 2), (0, 3), (1, 0), (1, 1)):
            store_rows(0, h, i)
        for c in (1, 2):
            quantize_w(1, 1, c)
            one_pass(1, 0, 1, c, c)
        round_y(0, 0, "vector")
        for t in range(PACK):
            maxout(1, 0, t)
            if t == 0:
                quantize_y(0, 0)
                store_codes(0, 0)
        round_y(0, 1, "vector")

        first_pieces(1, 1, LOW)
        for g, h, i in ((0, 1, 2), (0, 1, 3), (1, 0, 0), (1, 0, 1)):
            store_rows(g, h, i)
        quantize_y(0, 1)
        store_codes(0, 1)
        store_scales(0)
        second_pieces(1, 1, LOW)
        store_rows(1, 0, 2)
        store_rows(1, 0, 3)
        round_y(1, 0, "vector")
        first_pieces(1, 1, HIGH)
        round_y(1, 1, "vector", LOW)
        quantize_y(1, 0)
        store_codes(1, 0)
        store_rows(1, 1, 0)
        store_rows(1, 1, 1)
        quantize_y(1, 1, LOW)
        store_codes(1, 1, LOW)
        second_pieces(1, 1, HIGH)
        round_y(1, 1, "vector", HIGH)
        store_rows(1, 1, 2)
        store_rows(1, 1, 3, nc.scalar)
        quantize_y(1, 1, HIGH)
        store_codes(1, 1, HIGH)
        store_scales(1)
